import numpy as np
import ml_dtypes


def mxq(x, axis, fmt="e4m3"):
    dtype, down = {"e4m3": (ml_dtypes.float8_e4m3fn, 7), "e5m2": (ml_dtypes.float8_e5m2, 14)}[fmt]
    v = np.moveaxis(np.asarray(x, np.float32).astype(ml_dtypes.bfloat16).astype(np.float64), axis, -1)
    blocks = v.reshape(v.shape[:-1] + (-1, 32))
    amax = np.abs(blocks).max(-1, keepdims=True)
    byte = np.maximum(np.where(amax > 0, np.frexp(amax)[1] - 1 + 127, 0) - down, 1)
    scale = np.exp2(byte - 127.0)
    codes = (blocks / scale).astype(np.float32).astype(dtype).astype(np.float64)
    return np.moveaxis((codes * scale).reshape(v.shape), -1, axis)


WIDE = False


def mx_kscale(k):
    if not WIDE:
        return np.ones(k)
    levels = np.array([10, -10, 5, -5, 0])
    if k % 512:
        return np.exp2(np.random.permutation(np.resize(levels, k // 32))).repeat(32)
    a = np.empty((k // 512, 16))
    for p in range(k // 512):
        a[p, :8] = np.random.permutation(np.resize(levels, 8))
        for g in range(8):
            far = levels[np.abs(levels - a[p, g]) >= 10]
            a[p, g + 8] = far[np.random.randint(len(far))]
    return np.exp2(a.ravel()).repeat(32)


BF16 = ml_dtypes.bfloat16


def bf(x):
    return np.asarray(x, np.float32).astype(BF16)


def f64(x):
    return np.asarray(x).astype(np.float64)


E2M1 = np.array([0.0, 0.5, 1.0, 1.5, 2.0, 3.0, 4.0, 6.0, -0.0, -0.5, -1.0, -1.5, -2.0, -3.0, -4.0, -6.0])


def pack_weight(w, fmt):
    k, n = w.shape
    w = f64(bf(w)).reshape(k // 32, 32, n)
    amax = np.abs(w).max(1)
    if fmt == "e4m3":
        byte = np.frexp(amax)[1] - 1 + 127 - 7
    else:
        mant, ex = np.frexp(amax / 6.0)
        byte = np.where(mant > 0.5, ex, ex - 1) + 127
    byte = np.clip(np.where(amax > 0, byte, 1), 1, 254)
    scaled = (w * np.exp2(127.0 - byte)[:, None, :]).reshape(k, n).astype(np.float32)
    by_word = np.ascontiguousarray(scaled.reshape(k // 512, 128, 4, n).transpose(0, 1, 3, 2))
    if fmt == "e4m3":
        words = by_word.astype(ml_dtypes.float8_e4m3fn).view(np.uint8)
    else:
        c = by_word.astype(ml_dtypes.float4_e2m1fn).view(np.uint8) & 0xF
        words = c[..., 0::2] | (c[..., 1::2] << 4)
    return np.ascontiguousarray(words), np.ascontiguousarray(byte.astype(np.uint8).reshape(k // 512, 16, n))


def unpack_weight(words, scales, fmt):
    g, p, n, _ = words.shape
    if fmt == "e4m3":
        vals = np.ascontiguousarray(words).view(ml_dtypes.float8_e4m3fn).astype(np.float64)
    else:
        nib = np.empty((g, p, n, 4), np.uint8)
        nib[..., 0::2] = words & 0xF
        nib[..., 1::2] = words >> 4
        vals = E2M1[nib]
    vals = vals * np.repeat(np.exp2(scales.astype(np.float64) - 127.0), 8, axis=1)[..., None]
    return vals.transpose(0, 1, 3, 2).reshape(g * 512, n)
def pack4(w):
    words, scales = pack_weight(w, "e2m1")
    return words.reshape(words.shape[0], 128, -1), scales


def unpack4(words, scales):
    return unpack_weight(words.reshape(words.shape[0], 128, -1, 2), scales, "e2m1")


E4M3FN = np.array([(-1.0 if i & 128 else 1.0) * ((1.0 + (i & 7) / 8.0) * 2.0 ** (((i >> 3) & 15) - 7) if i & 120 else (i & 7) * 2.0 ** -9) for i in range(256)])


def e4m3fn_bytes(y):
    return np.clip(np.asarray(y, np.float64), -448.0, 448.0).astype(np.float32).astype(ml_dtypes.float8_e4m3fn).view(np.uint8)


def e4m3fn_values(b):
    return E4M3FN[b]

def planes(Y):
    n, m = Y.shape
    b = f64(bf(Y)).reshape(n // 32, 32, m)
    amax = np.abs(b).max(1)
    byte = np.clip(np.where(amax > 0, np.frexp(amax)[1] - 1 + 127 - 7, 1), 1, 254)
    codes = (b * np.exp2(127.0 - byte)[:, None, :]).reshape(n, m).astype(np.float32).astype(ml_dtypes.float8_e4m3fn).view(np.uint8)
    words = codes.reshape(n // 512, 128, 4, m).transpose(0, 1, 3, 2)
    return np.ascontiguousarray(words), np.ascontiguousarray(byte.astype(np.uint8).reshape(n // 512, 16, m))


T, K, J, F, N, B = 2048, 1024, 512, 512, 1024, 128
FP8_MAX = 448.0

def setup_inputs():
    r = np.random.randn
    s, u, t = mx_kscale(K), mx_kscale(J), mx_kscale(F)
    X = r(T, K) * s
    X_scale = (np.abs(X).reshape(T, K // B, B).max(axis=2) / FP8_MAX).astype(np.float32)
    X_bytes = e4m3fn_bytes(X / np.repeat(f64(X_scale), B, axis=1))
    G_words, G_scales = pack4(r(J, N) * u[:, None])
    return {
        "X_bytes": X_bytes, "X_scale": X_scale,
        "G_words": G_words, "G_scales": G_scales,
        "Wa": bf(r(K, F) / np.sqrt(K) / s[:, None]),
        "Wb": bf(r(K, F) / np.sqrt(K) / s[:, None]),
        "Va": bf(r(J, F) / np.sqrt(J) / u[:, None]),
        "Vb": bf(r(J, F) / np.sqrt(J) / u[:, None]),
        "phi_gain": bf((1 + 0.1 * r(1, F)) * t),
        "psi_gain": bf((1 + 0.1 * r(1, F)) / t),
        "goal_scale": bf(np.exp(0.8 * r(1, N)) * 10 / np.sqrt(F)),
    }

def reference(X_bytes, X_scale, G_words, G_scales, Wa, Wb, Va, Vb, phi_gain, psi_gain, goal_scale):
    X = e4m3fn_values(X_bytes) * np.repeat(f64(X_scale), B, axis=1)
    Xq = mxq(X, 1, "e4m3")
    G = unpack4(G_words, G_scales)
    a = Xq @ mxq(f64(Wa), 0, "e4m3")
    b = Xq @ mxq(f64(Wb), 0, "e4m3")
    phi = np.tanh(a) * (1 / (1 + np.exp(-b))) * f64(phi_gain)
    c = G.T @ mxq(f64(Va), 0, "e4m3")
    d = G.T @ mxq(f64(Vb), 0, "e4m3")
    psi = np.tanh(c) * (1 / (1 + np.exp(-d))) * f64(psi_gain)
    y = (mxq(phi, 1, "e4m3") @ mxq(psi, 1, "e4m3").T) * f64(goal_scale)
    words, scales = planes(y.T)
    return y, words, scales

@@ -1,0 +1,545 @@
+from contextlib import ExitStack
+
+import concourse.mybir as mybir
+from concourse.masks import make_identity
+
+T, K, J, F, N = 2048, 1024, 512, 512, 1024
+FLOPS = 2 * (2 * T * K * F + 2 * N * J * F + T * F * N)
+
+F32 = mybir.dt.float32
+BF16 = mybir.dt.bfloat16
+I32 = mybir.dt.int32
+U32 = mybir.dt.uint32
+U8 = mybir.dt.uint8
+FP8 = mybir.dt.float8_e4m3fn
+FP8X4 = mybir.dt.float8_e4m3fn_x4
+FP4X4 = mybir.dt.float4_e2m1fn_x4
+ACT = mybir.ActivationFunctionType
+MULT = mybir.AluOpType.mult
+
+P = 128
+PACK = 4
+K_PASS = P * PACK
+W = 256
+CHUNKS = T // W
+GOAL_GROUPS = N // W
+ROWS = W // P
+SCALE_BLOCK = 128
+LAST_SCALES = 2
+
+
+def tile_goal_conditioned_critic_b8_kernel(
+    tc, X_bytes, X_scale, G_words, G_scales, Wa, Wb, Va, Vb, phi_gain, psi_gain, goal_scale, out_0, out_1, out_2
+):
+    nc = tc.nc
+    with ExitStack() as ctx:
+        keep = ctx.enter_context(tc.tile_pool(name="keep", bufs=1))
+        work = ctx.enter_context(tc.tile_pool(name="work", bufs=2))
+        psum = ctx.enter_context(tc.psum_pool(name="psum", bufs=8))
+        ctx.enter_context(tc.manual_schedule())
+
+        x_raw, w_raw, w_grouped, w_codes, w_scales = {}, {}, {}, {}, {}
+        x_wide, x_bank, x_grouped, x_codes, x_scales = {}, {}, {}, {}, {}
+        gate_bank, tanh_part, sigmoid_part, feat_planes, feat_grouped = {}, {}, {}, {}, {}
+        phi_codes, phi_scales = {}, {}
+        y_bank, y_rows, y_half, yt_bank, yt_grouped, yt_codes = {}, {}, {}, {}, {}, {}
+
+        warm = keep.tile([P, 1], F32, name="warm")
+        nc.vector.memset(warm[:], 0.0)
+        nc.scalar.activation(out=warm[:], in_=warm[:], func=ACT.Sigmoid)
+
+        ident = keep.tile([P, P], F32, name="ident")
+        make_identity(nc, ident[:])
+        g_scales = keep.tile([P, N], U8, name="g_scales", align_bytes=64)
+        nc.vector.memset(g_scales[:].bitcast(I32), 0)
+
+        def load_x(c):
+            x_raw[c] = keep.tile([P, ROWS * K], U8, name="x_raw%d" % c)
+            nc.sync.dma_start(out=x_raw[c][:], in_=X_bytes[c * W : (c + 1) * W, :].rearrange("(p i) k -> p (i k)", i=ROWS))
+
+        weights = {"va": Va, "vb": Vb, "wa": Wa, "wb": Wb}
+
+        def load_w(name, g):
+            w_raw[name, g] = keep.tile([P, PACK, F], BF16, name="raw_%s%d" % (name, g))
+            nc.sync.dma_start(
+                out=w_raw[name, g][:],
+                in_=weights[name][g * K_PASS : (g + 1) * K_PASS, :].rearrange("(p j) f -> p j f", j=PACK),
+            )
+
+        x_scale_first = keep.tile([P, 1, ROWS * K // SCALE_BLOCK], F32, name="x_scale_first")
+        x_scale_rest = keep.tile([P, CHUNKS - 1, ROWS * K // SCALE_BLOCK], F32, name="x_scale_rest")
+        g_words = keep.tile([P, 2 * N], U8, name="g_words", align_bytes=64)
+        gain_raw = {"phi": keep.tile([P, PACK], BF16, name="phi_gain_raw"), "psi": keep.tile([P, PACK], BF16, name="psi_gain_raw")}
+        gain = {"phi": keep.tile([P, PACK], F32, name="phi_gain"), "psi": keep.tile([P, PACK], F32, name="psi_gain")}
+        goal_row = keep.tile([P, N], BF16, name="goal_row")
+
+        scale_rows = X_scale.rearrange("(c p i) j -> p c (i j)", p=P, i=ROWS)
+        load_x(0)
+        nc.sync.dma_start(out=x_scale_first[:], in_=scale_rows[:, 0:1, :])
+        load_w("va", 0)
+        for q in range(4):
+            nc.sync.dma_start(
+                out=g_scales[32 * q : 32 * q + 4, :].bitcast(I32), in_=G_scales[0, 4 * q : 4 * q + 4, :].bitcast(I32)
+            )
+        load_w("vb", 0)
+        load_w("wa", 0)
+        nc.sync.dma_start(out=g_words[:], in_=G_words[0])
+        load_x(1)
+        nc.sync.dma_start(out=x_scale_rest[:], in_=scale_rows[:, 1:, :])
+        load_w("wb", 0)
+        nc.sync.dma_start(out=gain_raw["psi"][:], in_=psi_gain.rearrange("o (p t) -> p (o t)", t=PACK))
+        nc.sync.dma_start(out=gain_raw["phi"][:], in_=phi_gain.rearrange("o (p t) -> p (o t)", t=PACK))
+        load_w("wa", 1)
+        load_w("wb", 1)
+        for c in range(2, CHUNKS):
+            load_x(c)
+        nc.sync.dma_start(out=goal_row[:], in_=goal_scale.rearrange("o n -> (o n)").partition_broadcast(P))
+
+        psi_codes = [keep.tile([P, N // 2], U32, name="psi_codes%d" % h, align_bytes=64) for h in range(2)]
+        psi_scales = [keep.tile([P, N // 2], U8, name="psi_scales%d" % h, align_bytes=64) for h in range(2)]
+        first_cols = (CHUNKS - LAST_SCALES) * W
+        yt_scales = [
+            keep.tile([P, 2, first_cols], U8, name="yt_scales_first", align_bytes=64),
+            keep.tile([P, 2, T - first_cols], U8, name="yt_scales_last", align_bytes=64),
+        ]
+
+        def group_w(name, g, on_scalar):
+            w_grouped[name, g] = work.tile([P, PACK * F], BF16, name="w_grouped", bufs=3, align_bytes=64)
+            dst = w_grouped[name, g][:].rearrange("p (t m j) -> p m j t", t=PACK, j=PACK)
+            src = w_raw[name, g][:].rearrange("p j (m t) -> p m j t", t=PACK)
+            if on_scalar:
+                nc.scalar.copy(out=dst, in_=src)
+            else:
+                nc.vector.tensor_copy(out=dst, in_=src)
+
+        def quantize_w(name, g):
+            w_codes[name, g] = keep.tile([P, F], U32, name="codes_%s%d" % (name, g), align_bytes=64)
+            w_scales[name, g] = keep.tile([P, F], U8, name="scales_%s%d" % (name, g), align_bytes=64)
+            nc.vector.quantize_mx(out=w_codes[name, g][:].bitcast(FP8X4), scales=w_scales[name, g][:], in_=w_grouped[name, g][:])
+
+        def widen_gain(name):
+            nc.vector.tensor_copy(out=gain[name][:], in_=gain_raw[name][:])
+
+        def widen_x(c, g, on_scalar=True):
+            for i in range(ROWS):
+                x_wide[c, g, i] = work.tile([P, K_PASS], BF16, name="x_wide", bufs=8)
+                for b in range(K_PASS // SCALE_BLOCK):
+                    j = (i * K + g * K_PASS) // SCALE_BLOCK + b
+                    dst = x_wide[c, g, i][:, b * SCALE_BLOCK : (b + 1) * SCALE_BLOCK]
+                    src = x_raw[c][:, j * SCALE_BLOCK : (j + 1) * SCALE_BLOCK].bitcast(FP8)
+                    scale = x_scale_first[:, 0, j : j + 1] if c == 0 else x_scale_rest[:, c - 1, j : j + 1]
+                    if on_scalar:
+                        nc.scalar.activation(out=dst, in_=src, func=ACT.Copy, scale=scale)
+                    else:
+                        nc.vector.tensor_scalar(out=dst, in0=src, scalar1=scale, scalar2=None, op0=MULT)
+
+        def turn_x(c, g):
+            x_bank[c, g] = psum.tile([P, ROWS, 2, P], F32, name="bank")
+            for i in range(ROWS):
+                words = x_wide[c, g, i][:].bitcast(F32)
+                for u in range(2):
+                    nc.tensor.transpose(x_bank[c, g][:, i, u, :], words[:, u : 2 * P : 2], ident[:])
+
+        def group_x(c, g, on_scalar=True):
+            if g == 0:
+                x_grouped[c] = work.tile([P, 2, ROWS, P, 2], F32, name="x_grouped", align_bytes=64)
+            copy = nc.scalar.copy if on_scalar else nc.vector.tensor_copy
+            copy(out=x_grouped[c][:, g], in_=x_bank[c, g][:].rearrange("p i u r -> p i r u"))
+
+        def quantize_x(c):
+            x_codes[c] = work.tile([P, 2 * W], U32, name="x_codes", bufs=3, align_bytes=64)
+            x_scales[c] = work.tile([P, 2 * W], U8, name="x_scales", bufs=3, align_bytes=64)
+            nc.vector.quantize_mx(
+                out=x_codes[c][:].bitcast(FP8X4),
+                scales=x_scales[c][:],
+                in_=x_grouped[c][:].rearrange("p g i r u -> p (g i r u)").bitcast(BF16),
+            )
+
+        def gate_matmuls(kind, c, h):
+            for name in ("va", "vb") if kind == "psi" else ("wa", "wb"):
+                bank = psum.tile([P, 2, W], F32, name="bank")
+                gate_bank[kind, c, h, name[1]] = bank
+                for s in range(2):
+                    cols = slice((2 * h + s) * P, (2 * h + s + 1) * P)
+                    passes = 1 if kind == "psi" else 2
+                    for g in range(passes):
+                        if kind == "psi":
+                            rhs = g_words[:, 2 * c * W : 2 * (c + 1) * W].bitcast(FP4X4)
+                            rhs_scale = g_scales[:, c * W : (c + 1) * W]
+                        else:
+                            rhs = x_codes[c][:, g * W : (g + 1) * W].bitcast(FP8X4)
+                            rhs_scale = x_scales[c][:, g * W : (g + 1) * W]
+                        nc.tensor.matmul_mx(
+                            out=bank[:, s, :],
+                            lhsT=w_codes[name, g][:, cols].bitcast(FP8X4),
+                            lhsT_scale=w_scales[name, g][:, cols],
+                            rhs=rhs,
+                            rhs_scale=rhs_scale,
+                            start=(g == 0),
+                            stop=(g == passes - 1),
+                        )
+
+        def gate_functions(kind, c, h):
+            tanh_part[kind, c, h] = work.tile([P, 2, W], F32, name="tanh_part", bufs=4)
+            sigmoid_part[kind, c, h] = work.tile([P, 2, W], F32, name="sigmoid_part", bufs=4)
+            nc.scalar.activation(out=tanh_part[kind, c, h][:], in_=gate_bank[kind, c, h, "a"][:], func=ACT.Tanh)
+            nc.scalar.activation(out=sigmoid_part[kind, c, h][:], in_=gate_bank[kind, c, h, "b"][:], func=ACT.Sigmoid)
+
+        def gate_product(kind, c, h):
+            if h == 0:
+                feat_planes[kind, c] = work.tile([P, PACK, W], BF16, name="feat_planes")
+            for s in range(2):
+                t = 2 * h + s
+                nc.vector.scalar_tensor_tensor(
+                    out=feat_planes[kind, c][:, t, :],
+                    in0=tanh_part[kind, c, h][:, s, :],
+                    scalar=gain[kind][:, t : t + 1],
+                    in1=sigmoid_part[kind, c, h][:, s, :],
+                    op0=MULT,
+                    op1=MULT,
+                )
+
+        def group_feat(kind, c, on_scalar=False):
+            feat_grouped[kind, c] = work.tile([P, W * PACK], BF16, name="feat_grouped", align_bytes=64)
+            copy = nc.scalar.copy if on_scalar else nc.vector.tensor_copy
+            copy(
+                out=feat_grouped[kind, c][:].rearrange("p (r i t) -> p r t i", i=4, t=PACK),
+                in_=feat_planes[kind, c][:].rearrange("p t (r i) -> p r t i", i=4),
+            )
+
+        def quantize_feat(kind, c):
+            if kind == "psi":
+                cols = slice((c % 2) * W, (c % 2 + 1) * W)
+                codes, scales = psi_codes[c // 2][:, cols], psi_scales[c // 2][:, cols]
+            else:
+                phi_codes[c] = work.tile([P, W], U32, name="phi_codes", align_bytes=64)
+                phi_scales[c] = work.tile([P, W], U8, name="phi_scales", align_bytes=64)
+                codes, scales = phi_codes[c][:], phi_scales[c][:]
+            nc.vector.quantize_mx(out=codes.bitcast(FP8X4), scales=scales, in_=feat_grouped[kind, c][:])
+
+        def y_matmuls(c, i):
+            for h in range(2):
+                y_bank[c, i, h] = psum.tile([P, N // 2], F32, name="bank")
+                nc.tensor.matmul_mx(
+                    out=y_bank[c, i, h][:],
+                    lhsT=phi_codes[c][:, i * P : (i + 1) * P].bitcast(FP8X4),
+                    lhsT_scale=phi_scales[c][:, i * P : (i + 1) * P],
+                    rhs=psi_codes[h][:].bitcast(FP8X4),
+                    rhs_scale=psi_scales[h][:],
+                    start=True,
+                    stop=True,
+                )
+
+        def scale_y(c, i):
+            y_rows[c, i] = work.tile([P, N], F32, name="y_rows", bufs=4)
+            for h in range(2):
+                cols = slice(h * N // 2, (h + 1) * N // 2)
+                nc.vector.tensor_tensor(out=y_rows[c, i][:, cols], in0=y_bank[c, i, h][:], in1=goal_row[:, cols], op=MULT)
+            nc.sync.dma_start(out=out_0[c * W : (c + 1) * W, :].rearrange("(p i) n -> p i n", i=ROWS)[:, i, :], in_=y_rows[c, i][:])
+
+        def round_y(c, i, on_scalar=False):
+            y_half[c, i] = work.tile([P, N], BF16, name="y_half", bufs=4)
+            copy = nc.scalar.copy if on_scalar else nc.vector.tensor_copy
+            copy(
+                out=y_half[c, i][:].rearrange("p (g u m e) -> p g m u e", g=2, u=2, e=2),
+                in_=y_rows[c, i][:].rearrange("p (g m u e) -> p g m u e", g=2, u=2, e=2),
+            )
+
+        def turn_y(c, g):
+            yt_bank[c, g] = psum.tile([P, ROWS, 2, P], F32, name="bank")
+            for i in range(ROWS):
+                words = y_half[c, i][:].bitcast(F32)
+                for u in range(2):
+                    first = (2 * g + u) * P
+                    nc.tensor.transpose(yt_bank[c, g][:, i, u, :], words[:, first : first + P], ident[:])
+
+        def group_y(c, g, on_scalar=True):
+            yt_grouped[c, g] = work.tile([P, P, ROWS, 2], F32, name="yt_grouped", bufs=4, align_bytes=64)
+            copy = nc.scalar.copy if on_scalar else nc.vector.tensor_copy
+            copy(out=yt_grouped[c, g][:], in_=yt_bank[c, g][:].rearrange("p i u r -> p r i u"))
+
+        def quantize_y(c, g):
+            if g == 0:
+                yt_codes[c] = work.tile([P, 2, W], U32, name="yt_codes", bufs=3, align_bytes=64)
+            part = int(c * W >= first_cols)
+            first = c * W - part * first_cols
+            nc.vector.quantize_mx(
+                out=yt_codes[c][:, g, :].bitcast(FP8X4),
+                scales=yt_scales[part][:, g, first : first + W],
+                in_=yt_grouped[c, g][:].rearrange("p r i u -> p (r i u)").bitcast(BF16),
+            )
+            if g == 1:
+                nc.sync.dma_start(
+                    out=out_1[:, :, c * W : (c + 1) * W, :].rearrange("g p m t -> p g (m t)").bitcast(I32),
+                    in_=yt_codes[c][:].bitcast(I32),
+                )
+                if (c + 1) * W in (first_cols, T):
+                    cols = slice(part * first_cols, (c + 1) * W)
+                    for q in range(4):
+                        nc.sync.dma_start(
+                            out=out_2[:, 4 * q : 4 * q + 4, cols].rearrange("g r m -> r g m").bitcast(I32),
+                            in_=yt_scales[part][32 * q : 32 * q + 4].bitcast(I32),
+                        )
+
+        group_w("va", 0, False)
+        quantize_w("va", 0)
+        group_w("vb", 0, False)
+        group_w("wa", 0, False)
+        quantize_w("vb", 0)
+        quantize_w("wa", 0)
+        widen_gain("psi")
+        group_w("wb", 0, False)
+        group_w("wa", 1, False)
+        group_w("wb", 1, False)
+        quantize_w("wb", 0)
+        widen_gain("phi")
+        widen_x(0, 0, True)
+        widen_x(0, 1, True)
+        widen_x(1, 0, True)
+        widen_x(1, 1, True)
+        quantize_w("wa", 1)
+        turn_x(0, 0)
+        turn_x(0, 1)
+        group_x(0, 0, True)
+        group_x(0, 1, True)
+        gate_matmuls("psi", 0, 0)
+        gate_matmuls("psi", 0, 1)
+        gate_functions("psi", 0, 0)
+        gate_functions("psi", 0, 1)
+        widen_x(2, 0, False)
+        widen_x(2, 1, False)
+        turn_x(1, 0)
+        turn_x(1, 1)
+        quantize_x(0)
+        gate_matmuls("psi", 1, 0)
+        group_x(1, 0, True)
+        gate_matmuls("psi", 1, 1)
+        group_x(1, 1, True)
+        gate_functions("psi", 1, 0)
+        gate_product("psi", 0, 0)
+        gate_functions("psi", 1, 1)
+        gate_product("psi", 0, 1)
+        quantize_w("wb", 1)
+        widen_x(3, 0, False)
+        widen_x(3, 1, False)
+        gate_matmuls("psi", 2, 0)
+        gate_matmuls("psi", 2, 1)
+        turn_x(2, 0)
+        turn_x(2, 1)
+        gate_functions("psi", 2, 0)
+        gate_product("psi", 1, 0)
+        quantize_x(1)
+        group_feat("psi", 0, False)
+        gate_functions("psi", 2, 1)
+        group_x(2, 0, True)
+        group_x(2, 1, True)
+        gate_product("psi", 1, 1)
+        quantize_feat("psi", 0)
+        widen_x(4, 0, True)
+        gate_matmuls("psi", 3, 0)
+        gate_matmuls("psi", 3, 1)
+        gate_functions("psi", 3, 0)
+        gate_product("psi", 2, 0)
+        widen_x(4, 1, False)
+        group_feat("psi", 1, False)
+        gate_functions("psi", 3, 1)
+        turn_x(3, 0)
+        turn_x(3, 1)
+        quantize_x(2)
+        gate_product("psi", 2, 1)
+        quantize_feat("psi", 1)
+        group_x(3, 0, True)
+        group_x(3, 1, True)
+        gate_matmuls("phi", 0, 0)
+        gate_product("psi", 3, 0)
+        widen_x(5, 0, False)
+        group_feat("psi", 2, False)
+        gate_functions("phi", 0, 0)
+        gate_matmuls("phi", 0, 1)
+        widen_x(5, 1, False)
+        gate_product("psi", 3, 1)
+        quantize_feat("psi", 2)
+        turn_x(4, 0)
+        turn_x(4, 1)
+        quantize_x(3)
+        gate_functions("phi", 0, 1)
+        group_x(4, 0, True)
+        gate_product("phi", 0, 0)
+        group_x(4, 1, True)
+        gate_matmuls("phi", 1, 0)
+        gate_product("phi", 0, 1)
+        gate_functions("phi", 1, 0)
+        group_feat("psi", 3, False)
+        gate_matmuls("phi", 1, 1)
+        widen_x(6, 0, False)
+        quantize_feat("psi", 3)
+        gate_functions("phi", 1, 1)
+        widen_x(6, 1, True)
+        gate_product("phi", 1, 0)
+        gate_matmuls("phi", 2, 0)
+        group_feat("phi", 0, False)
+        gate_product("phi", 1, 1)
+        turn_x(5, 0)
+        turn_x(5, 1)
+        quantize_x(4)
+        gate_functions("phi", 2, 0)
+        group_x(5, 0, True)
+        gate_matmuls("phi", 2, 1)
+        group_x(5, 1, True)
+        gate_functions("phi", 2, 1)
+        quantize_feat("phi", 0)
+        gate_product("phi", 2, 0)
+        gate_matmuls("phi", 3, 0)
+        widen_x(7, 0, False)
+        group_feat("phi", 1, False)
+        gate_product("phi", 2, 1)
+        gate_functions("phi", 3, 0)
+        widen_x(7, 1, True)
+        gate_matmuls("phi", 3, 1)
+        turn_x(6, 0)
+        turn_x(6, 1)
+        quantize_x(5)
+        gate_functions("phi", 3, 1)
+        group_x(6, 0, True)
+        group_x(6, 1, True)
+        quantize_feat("phi", 1)
+        gate_product("phi", 3, 0)
+        gate_matmuls("phi", 4, 0)
+        group_feat("phi", 2, False)
+        gate_product("phi", 3, 1)
+        gate_functions("phi", 4, 0)
+        y_matmuls(0, 0)
+        gate_matmuls("phi", 4, 1)
+        gate_functions("phi", 4, 1)
+        y_matmuls(0, 1)
+        scale_y(0, 0)
+        quantize_feat("phi", 2)
+        gate_product("phi", 4, 0)
+        turn_x(7, 0)
+        turn_x(7, 1)
+        gate_matmuls("phi", 5, 0)
+        quantize_x(6)
+        group_feat("phi", 3, True)
+        gate_product("phi", 4, 1)
+        scale_y(0, 1)
+        y_matmuls(1, 0)
+        gate_functions("phi", 5, 0)
+        group_x(7, 0, True)
+        group_x(7, 1, True)
+        gate_matmuls("phi", 5, 1)
+        y_matmuls(1, 1)
+        scale_y(1, 0)
+        gate_functions("phi", 5, 1)
+        round_y(0, 0, False)
+        scale_y(1, 1)
+        quantize_feat("phi", 3)
+        gate_product("phi", 5, 0)
+        y_matmuls(2, 0)
+        round_y(0, 1, True)
+        gate_matmuls("phi", 6, 0)
+        group_feat("phi", 4, True)
+        gate_product("phi", 5, 1)
+        gate_functions("phi", 6, 0)
+        gate_matmuls("phi", 6, 1)
+        y_matmuls(2, 1)
+        quantize_x(7)
+        scale_y(2, 0)
+        turn_y(0, 0)
+        turn_y(0, 1)
+        round_y(1, 0, False)
+        gate_functions("phi", 6, 1)
+        scale_y(2, 1)
+        y_matmuls(3, 0)
+        round_y(1, 1, True)
+        group_y(0, 0, True)
+        quantize_feat("phi", 4)
+        gate_product("phi", 6, 0)
+        gate_matmuls("phi", 7, 0)
+        group_feat("phi", 5, True)
+        gate_product("phi", 6, 1)
+        group_y(0, 1, True)
+        gate_functions("phi", 7, 0)
+        y_matmuls(3, 1)
+        scale_y(3, 0)
+        gate_matmuls("phi", 7, 1)
+        quantize_y(0, 0)
+        quantize_y(0, 1)
+        turn_y(1, 0)
+        turn_y(1, 1)
+        round_y(2, 0, False)
+        scale_y(3, 1)
+        y_matmuls(4, 0)
+        round_y(2, 1, True)
+        gate_functions("phi", 7, 1)
+        group_y(1, 0, True)
+        quantize_feat("phi", 5)
+        gate_product("phi", 7, 0)
+        group_y(1, 1, True)
+        group_feat("phi", 6, False)
+        gate_product("phi", 7, 1)
+        y_matmuls(4, 1)
+        scale_y(4, 0)
+        quantize_y(1, 0)
+        quantize_y(1, 1)
+        turn_y(2, 0)
+        turn_y(2, 1)
+        round_y(3, 0, True)
+        scale_y(4, 1)
+        y_matmuls(5, 0)
+        round_y(3, 1, True)
+        group_y(2, 0, True)
+        group_y(2, 1, True)
+        quantize_feat("phi", 6)
+        y_matmuls(5, 1)
+        scale_y(5, 0)
+        quantize_y(2, 0)
+        group_feat("phi", 7, True)
+        quantize_y(2, 1)
+        turn_y(3, 0)
+        turn_y(3, 1)
+        round_y(4, 0, True)
+        scale_y(5, 1)
+        y_matmuls(6, 0)
+        round_y(4, 1, False)
+        group_y(3, 0, True)
+        group_y(3, 1, True)
+        y_matmuls(6, 1)
+        scale_y(6, 0)
+        quantize_y(3, 0)
+        quantize_y(3, 1)
+        quantize_feat("phi", 7)
+        turn_y(4, 0)
+        turn_y(4, 1)
+        round_y(5, 0, True)
+        scale_y(6, 1)
+        y_matmuls(7, 0)
+        round_y(5, 1, True)
+        group_y(4, 0, True)
+        group_y(4, 1, True)
+        y_matmuls(7, 1)
+        scale_y(7, 0)
+        quantize_y(4, 0)
+        quantize_y(4, 1)
+        turn_y(5, 0)
+        turn_y(5, 1)
+        round_y(6, 0, True)
+        scale_y(7, 1)
+        round_y(6, 1, False)
+        group_y(5, 0, True)
+        group_y(5, 1, True)
+        quantize_y(5, 0)
+        quantize_y(5, 1)
+        turn_y(6, 0)
+        turn_y(6, 1)
+        round_y(7, 0, False)
+        round_y(7, 1, True)
+        group_y(6, 0, False)
+        group_y(6, 1, True)
+        quantize_y(6, 0)
+        quantize_y(6, 1)
+        turn_y(7, 0)
+        turn_y(7, 1)
+        group_y(7, 0, True)
+        group_y(7, 1, False)
+        quantize_y(7, 0)
+        quantize_y(7, 1)

@@ -16,6 +16,7 @@ FP8X4 = mybir.dt.float8_e4m3fn_x4
 FP4X4 = mybir.dt.float4_e2m1fn_x4
 ACT = mybir.ActivationFunctionType
 MULT = mybir.AluOpType.mult
+ADD = mybir.AluOpType.add
 
 P = 128
 PACK = 4
@@ -42,7 +43,8 @@ def tile_goal_conditioned_critic_b8_kernel(
         x_wide, x_bank, x_grouped, x_codes, x_scales = {}, {}, {}, {}, {}
         gate_bank, tanh_part, sigmoid_part, feat_planes, feat_grouped = {}, {}, {}, {}, {}
         phi_codes, phi_scales = {}, {}
-        y_bank, y_rows, y_half, yt_bank, yt_grouped, yt_codes = {}, {}, {}, {}, {}, {}
+        y_bank, y_half, yt_bank, yt_grouped = {}, {}, {}, {}
+        y_rows = keep.tile([P, CHUNKS * ROWS * N], F32, name="y_rows")
 
         warm = keep.tile([P, 1], F32, name="warm")
         nc.vector.memset(warm[:], 0.0)
@@ -74,26 +76,24 @@ def tile_goal_conditioned_critic_b8_kernel(
         goal_row = keep.tile([P, N], BF16, name="goal_row")
 
         scale_rows = X_scale.rearrange("(c p i) j -> p c (i j)", p=P, i=ROWS)
-        load_x(0)
-        nc.sync.dma_start(out=x_scale_first[:], in_=scale_rows[:, 0:1, :])
-        load_w("va", 0)
-        for q in range(4):
-            nc.sync.dma_start(
-                out=g_scales[32 * q : 32 * q + 4, :].bitcast(I32), in_=G_scales[0, 4 * q : 4 * q + 4, :].bitcast(I32)
-            )
-        load_w("vb", 0)
-        load_w("wa", 0)
-        nc.sync.dma_start(out=g_words[:], in_=G_words[0])
-        load_x(1)
-        nc.sync.dma_start(out=x_scale_rest[:], in_=scale_rows[:, 1:, :])
-        load_w("wb", 0)
-        nc.sync.dma_start(out=gain_raw["psi"][:], in_=psi_gain.rearrange("o (p t) -> p (o t)", t=PACK))
-        nc.sync.dma_start(out=gain_raw["phi"][:], in_=phi_gain.rearrange("o (p t) -> p (o t)", t=PACK))
-        load_w("wa", 1)
-        load_w("wb", 1)
-        for c in range(2, CHUNKS):
-            load_x(c)
-        nc.sync.dma_start(out=goal_row[:], in_=goal_scale.rearrange("o n -> (o n)").partition_broadcast(P))
+
+        def load_small(what):
+            if what == "scale_first":
+                nc.sync.dma_start(out=x_scale_first[:], in_=scale_rows[:, 0:1, :])
+            elif what == "scale_rest":
+                nc.sync.dma_start(out=x_scale_rest[:], in_=scale_rows[:, 1:, :])
+            elif what == "g_scales":
+                for q in range(4):
+                    nc.sync.dma_start(
+                        out=g_scales[32 * q : 32 * q + 4, :].bitcast(I32), in_=G_scales[0, 4 * q : 4 * q + 4, :].bitcast(I32)
+                    )
+            elif what == "g_words":
+                nc.sync.dma_start(out=g_words[:], in_=G_words[0])
+            elif what == "gains":
+                nc.sync.dma_start(out=gain_raw["psi"][:], in_=psi_gain.rearrange("o (p t) -> p (o t)", t=PACK))
+                nc.sync.dma_start(out=gain_raw["phi"][:], in_=phi_gain.rearrange("o (p t) -> p (o t)", t=PACK))
+            else:
+                nc.sync.dma_start(out=goal_row[:], in_=goal_scale.rearrange("o n -> (o n)").partition_broadcast(P))
 
         psi_codes = [keep.tile([P, N // 2], U32, name="psi_codes%d" % h, align_bytes=64) for h in range(2)]
         psi_scales = [keep.tile([P, N // 2], U8, name="psi_scales%d" % h, align_bytes=64) for h in range(2)]
@@ -231,27 +231,36 @@ def tile_goal_conditioned_critic_b8_kernel(
                 )
 
         def scale_y(c, i):
-            y_rows[c, i] = work.tile([P, N], F32, name="y_rows", bufs=4)
+            first = (c * ROWS + i) * N
             for h in range(2):
-                cols = slice(h * N // 2, (h + 1) * N // 2)
-                nc.vector.tensor_tensor(out=y_rows[c, i][:, cols], in0=y_bank[c, i, h][:], in1=goal_row[:, cols], op=MULT)
-            nc.sync.dma_start(out=out_0[c * W : (c + 1) * W, :].rearrange("(p i) n -> p i n", i=ROWS)[:, i, :], in_=y_rows[c, i][:])
-
-        def round_y(c, i, on_scalar=False):
-            y_half[c, i] = work.tile([P, N], BF16, name="y_half", bufs=4)
-            copy = nc.scalar.copy if on_scalar else nc.vector.tensor_copy
-            copy(
-                out=y_half[c, i][:].rearrange("p (g u m e) -> p g m u e", g=2, u=2, e=2),
-                in_=y_rows[c, i][:].rearrange("p (g m u e) -> p g m u e", g=2, u=2, e=2),
+                cols = slice(h * K_PASS, (h + 1) * K_PASS)
+                nc.vector.tensor_tensor(
+                    out=y_rows[:, first + cols.start : first + cols.stop], in0=y_bank[c, i, h][:], in1=goal_row[:, cols], op=MULT
+                )
+            nc.sync.dma_start(
+                out=out_0[c * W : (c + 1) * W, :].rearrange("(p i) n -> p i n", i=ROWS)[:, i, :], in_=y_rows[:, first : first + N]
             )
+
+        def round_y(c, i, engine):
+            r = c * ROWS + i
+            y_half[r] = work.tile([P, N], BF16, name="y_half", bufs=5)
+            first, last = max(r * N - K_PASS, 0), min(r * N + K_PASS, CHUNKS * ROWS * N)
+            dst = y_half[r][:, first - (r * N - K_PASS) : last - (r * N - K_PASS)]
+            src = y_rows[:, first:last]
+            if engine == 2:
+                nc.gpsimd.tensor_scalar(out=dst, in0=src, scalar1=1.0, scalar2=0.0, op0=MULT, op1=ADD)
+            elif engine == 1:
+                nc.scalar.copy(out=dst, in_=src)
+            else:
+                nc.vector.tensor_copy(out=dst, in_=src)
 
         def turn_y(c, g):
             yt_bank[c, g] = psum.tile([P, ROWS, 2, P], F32, name="bank")
             for i in range(ROWS):
-                words = y_half[c, i][:].bitcast(F32)
+                words = y_half[c * ROWS + i + g][:].bitcast(F32)
                 for u in range(2):
-                    first = (2 * g + u) * P
-                    nc.tensor.transpose(yt_bank[c, g][:, i, u, :], words[:, first : first + P], ident[:])
+                    first = (1 - g) * 2 * P
+                    nc.tensor.transpose(yt_bank[c, g][:, i, u, :], words[:, first + u : first + 2 * P : 2], ident[:])
 
         def group_y(c, g, on_scalar=True):
             yt_grouped[c, g] = work.tile([P, P, ROWS, 2], F32, name="yt_grouped", bufs=4, align_bytes=64)
@@ -259,287 +268,306 @@ def tile_goal_conditioned_critic_b8_kernel(
             copy(out=yt_grouped[c, g][:], in_=yt_bank[c, g][:].rearrange("p i u r -> p r i u"))
 
         def quantize_y(c, g):
-            if g == 0:
-                yt_codes[c] = work.tile([P, 2, W], U32, name="yt_codes", bufs=3, align_bytes=64)
+            yt_codes = work.tile([P, W], U32, name="yt_codes", bufs=6, align_bytes=64)
             part = int(c * W >= first_cols)
             first = c * W - part * first_cols
             nc.vector.quantize_mx(
-                out=yt_codes[c][:, g, :].bitcast(FP8X4),
+                out=yt_codes[:].bitcast(FP8X4),
                 scales=yt_scales[part][:, g, first : first + W],
                 in_=yt_grouped[c, g][:].rearrange("p r i u -> p (r i u)").bitcast(BF16),
             )
-            if g == 1:
-                nc.sync.dma_start(
-                    out=out_1[:, :, c * W : (c + 1) * W, :].rearrange("g p m t -> p g (m t)").bitcast(I32),
-                    in_=yt_codes[c][:].bitcast(I32),
-                )
-                if (c + 1) * W in (first_cols, T):
-                    cols = slice(part * first_cols, (c + 1) * W)
-                    for q in range(4):
-                        nc.sync.dma_start(
-                            out=out_2[:, 4 * q : 4 * q + 4, cols].rearrange("g r m -> r g m").bitcast(I32),
-                            in_=yt_scales[part][32 * q : 32 * q + 4].bitcast(I32),
-                        )
+            nc.sync.dma_start(
+                out=out_1[g, :, c * W : (c + 1) * W, :].rearrange("p m t -> p (m t)").bitcast(I32), in_=yt_codes[:].bitcast(I32)
+            )
+            if g == 1 and (c + 1) * W in (first_cols, T):
+                cols = slice(part * first_cols, (c + 1) * W)
+                for q in range(4):
+                    queue = nc.scalar if part == 1 and q < 3 else nc.sync
+                    queue.dma_start(
+                        out=out_2[:, 4 * q : 4 * q + 4, cols].rearrange("g r m -> r g m").bitcast(I32),
+                        in_=yt_scales[part][32 * q : 32 * q + 4].bitcast(I32),
+                    )
 
-        group_w("va", 0, False)
-        quantize_w("va", 0)
-        group_w("vb", 0, False)
-        group_w("wa", 0, False)
+        load_w("vb", 0)
+        load_small("gains")
+        load_w("va", 0)
+        load_w("wb", 0)
+        load_w("wa", 0)
+        load_small("g_words")
+        load_small("g_scales")
+        load_w("wa", 1)
+        load_small("scale_first")
+        group_w("vb", 0, 0)
+        group_w("va", 0, 0)
+        load_w("wb", 1)
+        load_x(0)
+        load_small("goal_row")
         quantize_w("vb", 0)
-        quantize_w("wa", 0)
+        load_x(1)
+        load_x(2)
+        group_w("wb", 0, 1)
+        load_x(3)
         widen_gain("psi")
-        group_w("wb", 0, False)
-        group_w("wa", 1, False)
-        group_w("wb", 1, False)
+        load_x(4)
+        quantize_w("va", 0)
+        load_small("scale_rest")
+        group_w("wa", 0, 0)
         quantize_w("wb", 0)
+        load_x(5)
+        quantize_w("wa", 0)
         widen_gain("phi")
-        widen_x(0, 0, True)
-        widen_x(0, 1, True)
-        widen_x(1, 0, True)
-        widen_x(1, 1, True)
-        quantize_w("wa", 1)
-        turn_x(0, 0)
-        turn_x(0, 1)
-        group_x(0, 0, True)
-        group_x(0, 1, True)
+        group_w("wa", 1, 0)
         gate_matmuls("psi", 0, 0)
         gate_matmuls("psi", 0, 1)
         gate_functions("psi", 0, 0)
-        gate_functions("psi", 0, 1)
-        widen_x(2, 0, False)
-        widen_x(2, 1, False)
-        turn_x(1, 0)
-        turn_x(1, 1)
-        quantize_x(0)
         gate_matmuls("psi", 1, 0)
-        group_x(1, 0, True)
         gate_matmuls("psi", 1, 1)
-        group_x(1, 1, True)
+        gate_functions("psi", 0, 1)
+        group_w("wb", 1, 0)
         gate_functions("psi", 1, 0)
         gate_product("psi", 0, 0)
-        gate_functions("psi", 1, 1)
-        gate_product("psi", 0, 1)
-        quantize_w("wb", 1)
-        widen_x(3, 0, False)
-        widen_x(3, 1, False)
         gate_matmuls("psi", 2, 0)
         gate_matmuls("psi", 2, 1)
-        turn_x(2, 0)
-        turn_x(2, 1)
+        gate_functions("psi", 1, 1)
+        widen_x(0, 0, 0)
+        load_x(6)
         gate_functions("psi", 2, 0)
+        gate_product("psi", 0, 1)
         gate_product("psi", 1, 0)
-        quantize_x(1)
-        group_feat("psi", 0, False)
-        gate_functions("psi", 2, 1)
-        group_x(2, 0, True)
-        group_x(2, 1, True)
-        gate_product("psi", 1, 1)
-        quantize_feat("psi", 0)
-        widen_x(4, 0, True)
+        widen_x(0, 1, 0)
         gate_matmuls("psi", 3, 0)
         gate_matmuls("psi", 3, 1)
+        gate_functions("psi", 2, 1)
+        widen_x(1, 0, 0)
+        group_feat("psi", 0, 0)
+        widen_x(1, 1, 1)
+        turn_x(0, 0)
+        turn_x(0, 1)
+        group_x(0, 0, 1)
         gate_functions("psi", 3, 0)
+        gate_product("psi", 1, 1)
         gate_product("psi", 2, 0)
-        widen_x(4, 1, False)
-        group_feat("psi", 1, False)
+        widen_x(2, 0, 0)
+        group_x(0, 1, 1)
+        quantize_w("wb", 1)
         gate_functions("psi", 3, 1)
-        turn_x(3, 0)
-        turn_x(3, 1)
-        quantize_x(2)
+        quantize_w("wa", 1)
+        group_feat("psi", 1, 0)
+        quantize_feat("psi", 0)
+        widen_x(2, 1, 1)
+        turn_x(1, 0)
+        turn_x(1, 1)
+        group_x(1, 0, 1)
+        quantize_x(0)
+        widen_x(3, 0, 0)
+        group_x(1, 1, 1)
+        load_x(7)
         gate_product("psi", 2, 1)
-        quantize_feat("psi", 1)
-        group_x(3, 0, True)
-        group_x(3, 1, True)
-        gate_matmuls("phi", 0, 0)
         gate_product("psi", 3, 0)
-        widen_x(5, 0, False)
-        group_feat("psi", 2, False)
+        widen_x(3, 1, 0)
+        turn_x(2, 0)
+        turn_x(2, 1)
+        group_x(2, 0, 1)
+        group_feat("psi", 2, 0)
+        quantize_x(1)
+        quantize_feat("psi", 1)
+        widen_x(4, 0, 1)
+        group_x(2, 1, 1)
+        gate_matmuls("phi", 0, 0)
         gate_functions("phi", 0, 0)
         gate_matmuls("phi", 0, 1)
-        widen_x(5, 1, False)
+        widen_x(4, 1, 0)
         gate_product("psi", 3, 1)
+        turn_x(3, 0)
+        turn_x(3, 1)
+        gate_functions("phi", 0, 1)
+        group_x(3, 0, 1)
+        quantize_x(2)
+        widen_x(5, 0, 0)
+        gate_matmuls("phi", 1, 0)
+        group_x(3, 1, 1)
+        gate_functions("phi", 1, 0)
+        group_feat("psi", 3, 0)
         quantize_feat("psi", 2)
+        gate_matmuls("phi", 1, 1)
+        gate_product("phi", 0, 0)
+        gate_functions("phi", 1, 1)
+        widen_x(5, 1, 1)
         turn_x(4, 0)
         turn_x(4, 1)
+        group_x(4, 0, 1)
         quantize_x(3)
-        gate_functions("phi", 0, 1)
-        group_x(4, 0, True)
-        gate_product("phi", 0, 0)
-        group_x(4, 1, True)
-        gate_matmuls("phi", 1, 0)
-        gate_product("phi", 0, 1)
-        gate_functions("phi", 1, 0)
-        group_feat("psi", 3, False)
-        gate_matmuls("phi", 1, 1)
-        widen_x(6, 0, False)
-        quantize_feat("psi", 3)
-        gate_functions("phi", 1, 1)
-        widen_x(6, 1, True)
-        gate_product("phi", 1, 0)
         gate_matmuls("phi", 2, 0)
-        group_feat("phi", 0, False)
-        gate_product("phi", 1, 1)
+        gate_product("phi", 0, 1)
+        gate_functions("phi", 2, 0)
+        widen_x(6, 0, 0)
+        group_x(4, 1, 0)
+        group_feat("phi", 0, 0)
+        gate_matmuls("phi", 2, 1)
+        gate_product("phi", 1, 0)
+        gate_functions("phi", 2, 1)
+        quantize_feat("psi", 3)
+        widen_x(6, 1, 0)
         turn_x(5, 0)
         turn_x(5, 1)
-        quantize_x(4)
-        gate_functions("phi", 2, 0)
-        group_x(5, 0, True)
-        gate_matmuls("phi", 2, 1)
-        group_x(5, 1, True)
-        gate_functions("phi", 2, 1)
-        quantize_feat("phi", 0)
-        gate_product("phi", 2, 0)
         gate_matmuls("phi", 3, 0)
-        widen_x(7, 0, False)
-        group_feat("phi", 1, False)
-        gate_product("phi", 2, 1)
+        group_x(5, 0, 1)
+        gate_product("phi", 1, 1)
         gate_functions("phi", 3, 0)
-        widen_x(7, 1, True)
+        quantize_x(4)
+        quantize_feat("phi", 0)
+        group_feat("phi", 1, 0)
+        widen_x(7, 0, 1)
         gate_matmuls("phi", 3, 1)
-        turn_x(6, 0)
-        turn_x(6, 1)
-        quantize_x(5)
-        gate_functions("phi", 3, 1)
-        group_x(6, 0, True)
-        group_x(6, 1, True)
-        quantize_feat("phi", 1)
-        gate_product("phi", 3, 0)
-        gate_matmuls("phi", 4, 0)
-        group_feat("phi", 2, False)
-        gate_product("phi", 3, 1)
-        gate_functions("phi", 4, 0)
+        group_x(5, 1, 1)
         y_matmuls(0, 0)
-        gate_matmuls("phi", 4, 1)
-        gate_functions("phi", 4, 1)
-        y_matmuls(0, 1)
+        gate_product("phi", 2, 0)
+        gate_functions("phi", 3, 1)
+        gate_matmuls("phi", 4, 0)
         scale_y(0, 0)
+        widen_x(7, 1, 1)
+        turn_x(6, 0)
+        gate_product("phi", 2, 1)
+        gate_functions("phi", 4, 0)
+        turn_x(6, 1)
+        quantize_feat("phi", 1)
+        group_feat("phi", 2, 0)
+        group_x(6, 0, 1)
+        y_matmuls(0, 1)
+        quantize_x(5)
+        gate_matmuls("phi", 4, 1)
+        y_matmuls(1, 0)
+        group_x(6, 1, 1)
+        gate_product("phi", 3, 0)
+        gate_functions("phi", 4, 1)
+        scale_y(0, 1)
+        round_y(0, 0, 1)
+        scale_y(1, 0)
+        gate_matmuls("phi", 5, 0)
+        gate_product("phi", 3, 1)
+        gate_functions("phi", 5, 0)
         quantize_feat("phi", 2)
-        gate_product("phi", 4, 0)
+        y_matmuls(1, 1)
+        group_feat("phi", 3, 1)
         turn_x(7, 0)
         turn_x(7, 1)
-        gate_matmuls("phi", 5, 0)
-        quantize_x(6)
-        group_feat("phi", 3, True)
-        gate_product("phi", 4, 1)
-        scale_y(0, 1)
-        y_matmuls(1, 0)
-        gate_functions("phi", 5, 0)
-        group_x(7, 0, True)
-        group_x(7, 1, True)
-        gate_matmuls("phi", 5, 1)
-        y_matmuls(1, 1)
-        scale_y(1, 0)
-        gate_functions("phi", 5, 1)
-        round_y(0, 0, False)
-        scale_y(1, 1)
-        quantize_feat("phi", 3)
-        gate_product("phi", 5, 0)
         y_matmuls(2, 0)
-        round_y(0, 1, True)
-        gate_matmuls("phi", 6, 0)
-        group_feat("phi", 4, True)
-        gate_product("phi", 5, 1)
-        gate_functions("phi", 6, 0)
-        gate_matmuls("phi", 6, 1)
-        y_matmuls(2, 1)
-        quantize_x(7)
+        gate_matmuls("phi", 5, 1)
+        group_x(7, 0, 1)
+        quantize_x(6)
+        round_y(0, 1, 2)
+        gate_product("phi", 4, 0)
+        group_x(7, 1, 1)
+        gate_functions("phi", 5, 1)
+        scale_y(1, 1)
+        round_y(1, 0, 1)
         scale_y(2, 0)
+        gate_matmuls("phi", 6, 0)
+        gate_product("phi", 4, 1)
+        gate_functions("phi", 6, 0)
+        quantize_feat("phi", 3)
+        y_matmuls(2, 1)
+        group_feat("phi", 4, 0)
         turn_y(0, 0)
-        turn_y(0, 1)
-        round_y(1, 0, False)
-        gate_functions("phi", 6, 1)
-        scale_y(2, 1)
         y_matmuls(3, 0)
-        round_y(1, 1, True)
-        group_y(0, 0, True)
-        quantize_feat("phi", 4)
-        gate_product("phi", 6, 0)
-        gate_matmuls("phi", 7, 0)
-        group_feat("phi", 5, True)
-        gate_product("phi", 6, 1)
-        group_y(0, 1, True)
-        gate_functions("phi", 7, 0)
-        y_matmuls(3, 1)
+        gate_matmuls("phi", 6, 1)
+        round_y(1, 1, 2)
+        group_y(0, 0, 1)
+        quantize_x(7)
+        gate_product("phi", 5, 0)
+        gate_functions("phi", 6, 1)
+        turn_y(0, 1)
+        scale_y(2, 1)
+        round_y(2, 0, 1)
+        group_y(0, 1, 1)
         scale_y(3, 0)
+        gate_matmuls("phi", 7, 0)
+        gate_product("phi", 5, 1)
+        gate_functions("phi", 7, 0)
+        quantize_feat("phi", 4)
+        y_matmuls(3, 1)
+        group_feat("phi", 5, 1)
+        turn_y(1, 0)
+        y_matmuls(4, 0)
         gate_matmuls("phi", 7, 1)
+        round_y(2, 1, 2)
+        group_y(1, 0, 1)
+        gate_product("phi", 6, 0)
+        turn_y(1, 1)
+        gate_functions("phi", 7, 1)
+        scale_y(3, 1)
+        round_y(3, 0, 1)
+        group_y(1, 1, 1)
+        scale_y(4, 0)
         quantize_y(0, 0)
         quantize_y(0, 1)
-        turn_y(1, 0)
-        turn_y(1, 1)
-        round_y(2, 0, False)
-        scale_y(3, 1)
-        y_matmuls(4, 0)
-        round_y(2, 1, True)
-        gate_functions("phi", 7, 1)
-        group_y(1, 0, True)
-        quantize_feat("phi", 5)
-        gate_product("phi", 7, 0)
-        group_y(1, 1, True)
-        group_feat("phi", 6, False)
-        gate_product("phi", 7, 1)
+        gate_product("phi", 6, 1)
         y_matmuls(4, 1)
-        scale_y(4, 0)
+        quantize_feat("phi", 5)
+        turn_y(2, 0)
+        group_feat("phi", 6, 1)
+        y_matmuls(5, 0)
+        round_y(3, 1, 2)
+        group_y(2, 0, 1)
+        turn_y(2, 1)
+        gate_product("phi", 7, 0)
+        scale_y(4, 1)
+        round_y(4, 0, 1)
+        group_y(2, 1, 1)
+        scale_y(5, 0)
         quantize_y(1, 0)
         quantize_y(1, 1)
-        turn_y(2, 0)
-        turn_y(2, 1)
-        round_y(3, 0, True)
-        scale_y(4, 1)
-        y_matmuls(5, 0)
-        round_y(3, 1, True)
-        group_y(2, 0, True)
-        group_y(2, 1, True)
-        quantize_feat("phi", 6)
+        gate_product("phi", 7, 1)
         y_matmuls(5, 1)
-        scale_y(5, 0)
-        quantize_y(2, 0)
-        group_feat("phi", 7, True)
-        quantize_y(2, 1)
+        quantize_feat("phi", 6)
         turn_y(3, 0)
-        turn_y(3, 1)
-        round_y(4, 0, True)
-        scale_y(5, 1)
         y_matmuls(6, 0)
-        round_y(4, 1, False)
-        group_y(3, 0, True)
-        group_y(3, 1, True)
-        y_matmuls(6, 1)
+        group_feat("phi", 7, 1)
+        round_y(4, 1, 2)
+        group_y(3, 0, 1)
+        turn_y(3, 1)
+        scale_y(5, 1)
+        round_y(5, 0, 1)
+        group_y(3, 1, 1)
         scale_y(6, 0)
+        quantize_y(2, 0)
+        quantize_y(2, 1)
+        y_matmuls(6, 1)
+        turn_y(4, 0)
+        quantize_feat("phi", 7)
+        y_matmuls(7, 0)
+        round_y(5, 1, 2)
+        group_y(4, 0, 1)
+        turn_y(4, 1)
+        scale_y(6, 1)
+        round_y(6, 0, 1)
+        group_y(4, 1, 1)
+        scale_y(7, 0)
         quantize_y(3, 0)
         quantize_y(3, 1)
-        quantize_feat("phi", 7)
-        turn_y(4, 0)
-        turn_y(4, 1)
-        round_y(5, 0, True)
-        scale_y(6, 1)
-        y_matmuls(7, 0)
-        round_y(5, 1, True)
-        group_y(4, 0, True)
-        group_y(4, 1, True)
         y_matmuls(7, 1)
-        scale_y(7, 0)
+        turn_y(5, 0)
+        round_y(6, 1, 2)
+        group_y(5, 0, 1)
+        turn_y(5, 1)
+        scale_y(7, 1)
+        round_y(7, 0, 0)
+        group_y(5, 1, 1)
         quantize_y(4, 0)
         quantize_y(4, 1)
-        turn_y(5, 0)
-        turn_y(5, 1)
-        round_y(6, 0, True)
-        scale_y(7, 1)
-        round_y(6, 1, False)
-        group_y(5, 0, True)
-        group_y(5, 1, True)
+        turn_y(6, 0)
+        round_y(7, 1, 1)
+        group_y(6, 0, 1)
+        turn_y(6, 1)
+        round_y(8, 0, 1)
+        group_y(6, 1, 1)
         quantize_y(5, 0)
         quantize_y(5, 1)
-        turn_y(6, 0)
-        turn_y(6, 1)
-        round_y(7, 0, False)
-        round_y(7, 1, True)
-        group_y(6, 0, False)
-        group_y(6, 1, True)
+        turn_y(7, 0)
+        group_y(7, 0, 0)
+        turn_y(7, 1)
+        group_y(7, 1, 1)
         quantize_y(6, 0)
         quantize_y(6, 1)
-        turn_y(7, 0)
-        turn_y(7, 1)
-        group_y(7, 0, True)
-        group_y(7, 1, False)
         quantize_y(7, 0)
         quantize_y(7, 1)

@@ -43,6 +43,7 @@ def tile_goal_conditioned_critic_b8_kernel(
         x_wide, x_bank, x_grouped, x_codes, x_scales = {}, {}, {}, {}, {}
         gate_bank, tanh_part, sigmoid_part, feat_planes, feat_grouped = {}, {}, {}, {}, {}
         phi_codes, phi_scales = {}, {}
+        y_sorted = {}
         y_bank, y_half, yt_bank, yt_grouped = {}, {}, {}, {}
         y_rows = keep.tile([P, CHUNKS * ROWS * N], F32, name="y_rows")
 
@@ -249,10 +250,13 @@ def tile_goal_conditioned_critic_b8_kernel(
             src = y_rows[:, first:last]
             if engine == 2:
                 nc.gpsimd.tensor_scalar(out=dst, in0=src, scalar1=1.0, scalar2=0.0, op0=MULT, op1=ADD)
-            elif engine == 1:
-                nc.scalar.copy(out=dst, in_=src)
             else:
-                nc.vector.tensor_copy(out=dst, in_=src)
+                copy = nc.scalar.copy if engine == 1 else nc.vector.tensor_copy
+                copy(
+                    out=dst.rearrange("p (h u m e) -> p h m u e", u=2, m=P, e=2),
+                    in_=src.rearrange("p (h m u e) -> p h m u e", u=2, m=P, e=2),
+                )
+            y_sorted[r] = engine != 2
 
         def turn_y(c, g):
             yt_bank[c, g] = psum.tile([P, ROWS, 2, P], F32, name="bank")
@@ -260,7 +264,11 @@ def tile_goal_conditioned_critic_b8_kernel(
                 words = y_half[c * ROWS + i + g][:].bitcast(F32)
                 for u in range(2):
                     first = (1 - g) * 2 * P
-                    nc.tensor.transpose(yt_bank[c, g][:, i, u, :], words[:, first + u : first + 2 * P : 2], ident[:])
+                    if y_sorted[c * ROWS + i + g]:
+                        src = words[:, first + u * P : first + (u + 1) * P]
+                    else:
+                        src = words[:, first + u : first + 2 * P : 2]
+                    nc.tensor.transpose(yt_bank[c, g][:, i, u, :], src, ident[:])
 
         def group_y(c, g, on_scalar=True):
             yt_grouped[c, g] = work.tile([P, P, ROWS, 2], F32, name="yt_grouped", bufs=4, align_bytes=64)
@@ -290,284 +298,284 @@ def tile_goal_conditioned_critic_b8_kernel(
 
         load_w("vb", 0)
         load_small("gains")
+        load_small("scale_first")
+        load_x(0)
         load_w("va", 0)
         load_w("wb", 0)
         load_w("wa", 0)
         load_small("g_words")
         load_small("g_scales")
         load_w("wa", 1)
-        load_small("scale_first")
-        group_w("vb", 0, 0)
-        group_w("va", 0, 0)
-        load_w("wb", 1)
-        load_x(0)
-        load_small("goal_row")
-        quantize_w("vb", 0)
+        load_small("scale_rest")
         load_x(1)
         load_x(2)
-        group_w("wb", 0, 1)
+        load_w("wb", 1)
         load_x(3)
-        widen_gain("psi")
         load_x(4)
-        quantize_w("va", 0)
-        load_small("scale_rest")
-        group_w("wa", 0, 0)
-        quantize_w("wb", 0)
         load_x(5)
-        quantize_w("wa", 0)
+        load_x(6)
+        load_x(7)
+        load_small("goal_row")
+        group_w("vb", 0, 0)
+        quantize_w("vb", 0)
+        widen_x(0, 0, 1)
+        group_w("va", 0, 0)
+        widen_x(0, 1, 1)
+        group_w("wb", 0, 1)
+        widen_gain("psi")
+        quantize_w("va", 0)
+        group_w("wa", 0, 0)
         widen_gain("phi")
-        group_w("wa", 1, 0)
+        quantize_w("wa", 0)
+        quantize_w("wb", 0)
         gate_matmuls("psi", 0, 0)
         gate_matmuls("psi", 0, 1)
         gate_functions("psi", 0, 0)
-        gate_matmuls("psi", 1, 0)
-        gate_matmuls("psi", 1, 1)
         gate_functions("psi", 0, 1)
-        group_w("wb", 1, 0)
-        gate_functions("psi", 1, 0)
+        group_w("wa", 1, 0)
+        gate_matmuls("psi", 1, 0)
         gate_product("psi", 0, 0)
-        gate_matmuls("psi", 2, 0)
-        gate_matmuls("psi", 2, 1)
+        gate_matmuls("psi", 1, 1)
+        gate_functions("psi", 1, 0)
         gate_functions("psi", 1, 1)
-        widen_x(0, 0, 0)
-        load_x(6)
-        gate_functions("psi", 2, 0)
         gate_product("psi", 0, 1)
-        gate_product("psi", 1, 0)
-        widen_x(0, 1, 0)
-        gate_matmuls("psi", 3, 0)
-        gate_matmuls("psi", 3, 1)
-        gate_functions("psi", 2, 1)
+        group_w("wb", 1, 0)
         widen_x(1, 0, 0)
-        group_feat("psi", 0, 0)
-        widen_x(1, 1, 1)
+        gate_matmuls("psi", 2, 0)
+        gate_product("psi", 1, 0)
+        gate_matmuls("psi", 2, 1)
+        gate_functions("psi", 2, 0)
+        gate_functions("psi", 2, 1)
+        gate_product("psi", 1, 1)
+        widen_x(1, 1, 0)
         turn_x(0, 0)
         turn_x(0, 1)
+        group_feat("psi", 0, 0)
         group_x(0, 0, 1)
-        gate_functions("psi", 3, 0)
-        gate_product("psi", 1, 1)
-        gate_product("psi", 2, 0)
-        widen_x(2, 0, 0)
         group_x(0, 1, 1)
-        quantize_w("wb", 1)
-        gate_functions("psi", 3, 1)
+        widen_x(2, 0, 0)
         quantize_w("wa", 1)
-        group_feat("psi", 1, 0)
+        gate_matmuls("psi", 3, 0)
+        gate_product("psi", 2, 0)
+        gate_matmuls("psi", 3, 1)
+        gate_functions("psi", 3, 0)
+        quantize_x(0)
+        gate_functions("psi", 3, 1)
         quantize_feat("psi", 0)
+        gate_product("psi", 2, 1)
         widen_x(2, 1, 1)
+        quantize_w("wb", 1)
         turn_x(1, 0)
         turn_x(1, 1)
         group_x(1, 0, 1)
-        quantize_x(0)
-        widen_x(3, 0, 0)
         group_x(1, 1, 1)
-        load_x(7)
-        gate_product("psi", 2, 1)
-        gate_product("psi", 3, 0)
+        widen_x(3, 0, 0)
+        group_feat("psi", 1, 0)
+        quantize_x(1)
         widen_x(3, 1, 0)
         turn_x(2, 0)
         turn_x(2, 1)
-        group_x(2, 0, 1)
-        group_feat("psi", 2, 0)
-        quantize_x(1)
+        gate_product("psi", 3, 0)
         quantize_feat("psi", 1)
-        widen_x(4, 0, 1)
+        group_x(2, 0, 1)
         group_x(2, 1, 1)
-        gate_matmuls("phi", 0, 0)
-        gate_functions("phi", 0, 0)
-        gate_matmuls("phi", 0, 1)
-        widen_x(4, 1, 0)
         gate_product("psi", 3, 1)
+        widen_x(4, 0, 1)
+        group_feat("psi", 2, 0)
+        quantize_x(2)
+        widen_x(4, 1, 0)
+        gate_matmuls("phi", 0, 0)
         turn_x(3, 0)
         turn_x(3, 1)
-        gate_functions("phi", 0, 1)
+        gate_functions("phi", 0, 0)
         group_x(3, 0, 1)
-        quantize_x(2)
-        widen_x(5, 0, 0)
-        gate_matmuls("phi", 1, 0)
         group_x(3, 1, 1)
-        gate_functions("phi", 1, 0)
-        group_feat("psi", 3, 0)
+        widen_x(5, 0, 0)
+        gate_matmuls("phi", 0, 1)
         quantize_feat("psi", 2)
-        gate_matmuls("phi", 1, 1)
+        gate_functions("phi", 0, 1)
+        gate_matmuls("phi", 1, 0)
+        quantize_x(3)
         gate_product("phi", 0, 0)
-        gate_functions("phi", 1, 1)
-        widen_x(5, 1, 1)
+        widen_x(5, 1, 0)
+        gate_functions("phi", 1, 0)
         turn_x(4, 0)
         turn_x(4, 1)
-        group_x(4, 0, 1)
-        quantize_x(3)
-        gate_matmuls("phi", 2, 0)
+        group_feat("psi", 3, 0)
+        gate_matmuls("phi", 1, 1)
         gate_product("phi", 0, 1)
-        gate_functions("phi", 2, 0)
+        group_x(4, 0, 1)
+        group_x(4, 1, 1)
         widen_x(6, 0, 0)
-        group_x(4, 1, 0)
-        group_feat("phi", 0, 0)
-        gate_matmuls("phi", 2, 1)
+        gate_functions("phi", 1, 1)
+        gate_matmuls("phi", 2, 0)
         gate_product("phi", 1, 0)
-        gate_functions("phi", 2, 1)
+        gate_functions("phi", 2, 0)
+        quantize_x(4)
         quantize_feat("psi", 3)
-        widen_x(6, 1, 0)
+        widen_x(6, 1, 1)
+        gate_matmuls("phi", 2, 1)
+        gate_product("phi", 1, 1)
         turn_x(5, 0)
         turn_x(5, 1)
-        gate_matmuls("phi", 3, 0)
+        group_feat("phi", 0, 0)
+        gate_functions("phi", 2, 1)
         group_x(5, 0, 1)
-        gate_product("phi", 1, 1)
-        gate_functions("phi", 3, 0)
-        quantize_x(4)
-        quantize_feat("phi", 0)
-        group_feat("phi", 1, 0)
-        widen_x(7, 0, 1)
-        gate_matmuls("phi", 3, 1)
         group_x(5, 1, 1)
-        y_matmuls(0, 0)
+        gate_matmuls("phi", 3, 0)
+        widen_x(7, 0, 0)
         gate_product("phi", 2, 0)
-        gate_functions("phi", 3, 1)
-        gate_matmuls("phi", 4, 0)
-        scale_y(0, 0)
-        widen_x(7, 1, 1)
-        turn_x(6, 0)
+        quantize_feat("phi", 0)
+        gate_functions("phi", 3, 0)
+        gate_matmuls("phi", 3, 1)
         gate_product("phi", 2, 1)
-        gate_functions("phi", 4, 0)
-        turn_x(6, 1)
-        quantize_feat("phi", 1)
-        group_feat("phi", 2, 0)
-        group_x(6, 0, 1)
-        y_matmuls(0, 1)
+        y_matmuls(0, 0)
+        group_feat("phi", 1, 1)
         quantize_x(5)
-        gate_matmuls("phi", 4, 1)
-        y_matmuls(1, 0)
-        group_x(6, 1, 1)
+        gate_functions("phi", 3, 1)
+        widen_x(7, 1, 1)
+        scale_y(0, 0)
+        gate_matmuls("phi", 4, 0)
+        turn_x(6, 0)
+        turn_x(6, 1)
         gate_product("phi", 3, 0)
+        quantize_feat("phi", 1)
+        gate_functions("phi", 4, 0)
+        group_x(6, 0, 1)
+        group_x(6, 1, 1)
+        y_matmuls(0, 1)
+        y_matmuls(1, 0)
+        gate_matmuls("phi", 4, 1)
+        gate_product("phi", 3, 1)
+        group_feat("phi", 2, 0)
         gate_functions("phi", 4, 1)
         scale_y(0, 1)
-        round_y(0, 0, 1)
         scale_y(1, 0)
         gate_matmuls("phi", 5, 0)
-        gate_product("phi", 3, 1)
-        gate_functions("phi", 5, 0)
+        quantize_x(6)
+        gate_product("phi", 4, 0)
         quantize_feat("phi", 2)
-        y_matmuls(1, 1)
-        group_feat("phi", 3, 1)
+        gate_functions("phi", 5, 0)
         turn_x(7, 0)
+        round_y(0, 0, 1)
         turn_x(7, 1)
+        y_matmuls(1, 1)
         y_matmuls(2, 0)
         gate_matmuls("phi", 5, 1)
+        gate_product("phi", 4, 1)
         group_x(7, 0, 1)
-        quantize_x(6)
-        round_y(0, 1, 2)
-        gate_product("phi", 4, 0)
         group_x(7, 1, 1)
+        round_y(0, 1, 2)
+        group_feat("phi", 3, 1)
         gate_functions("phi", 5, 1)
         scale_y(1, 1)
-        round_y(1, 0, 1)
         scale_y(2, 0)
         gate_matmuls("phi", 6, 0)
-        gate_product("phi", 4, 1)
-        gate_functions("phi", 6, 0)
+        gate_product("phi", 5, 0)
         quantize_feat("phi", 3)
+        gate_functions("phi", 6, 0)
+        round_y(1, 0, 0)
         y_matmuls(2, 1)
-        group_feat("phi", 4, 0)
         turn_y(0, 0)
+        quantize_x(7)
         y_matmuls(3, 0)
         gate_matmuls("phi", 6, 1)
-        round_y(1, 1, 2)
-        group_y(0, 0, 1)
-        quantize_x(7)
-        gate_product("phi", 5, 0)
-        gate_functions("phi", 6, 1)
-        turn_y(0, 1)
-        scale_y(2, 1)
-        round_y(2, 0, 1)
-        group_y(0, 1, 1)
-        scale_y(3, 0)
-        gate_matmuls("phi", 7, 0)
         gate_product("phi", 5, 1)
-        gate_functions("phi", 7, 0)
+        round_y(1, 1, 2)
+        group_feat("phi", 4, 1)
+        gate_functions("phi", 6, 1)
+        scale_y(2, 1)
+        scale_y(3, 0)
+        turn_y(0, 1)
+        gate_matmuls("phi", 7, 0)
+        group_y(0, 0, 1)
+        gate_product("phi", 6, 0)
         quantize_feat("phi", 4)
+        gate_functions("phi", 7, 0)
+        round_y(2, 0, 1)
         y_matmuls(3, 1)
-        group_feat("phi", 5, 1)
         turn_y(1, 0)
         y_matmuls(4, 0)
+        group_y(0, 1, 1)
         gate_matmuls("phi", 7, 1)
+        gate_product("phi", 6, 1)
         round_y(2, 1, 2)
-        group_y(1, 0, 1)
-        gate_product("phi", 6, 0)
-        turn_y(1, 1)
+        group_feat("phi", 5, 1)
         gate_functions("phi", 7, 1)
         scale_y(3, 1)
-        round_y(3, 0, 1)
-        group_y(1, 1, 1)
         scale_y(4, 0)
+        turn_y(1, 1)
+        group_y(1, 0, 1)
         quantize_y(0, 0)
         quantize_y(0, 1)
-        gate_product("phi", 6, 1)
-        y_matmuls(4, 1)
-        quantize_feat("phi", 5)
-        turn_y(2, 0)
-        group_feat("phi", 6, 1)
-        y_matmuls(5, 0)
-        round_y(3, 1, 2)
-        group_y(2, 0, 1)
-        turn_y(2, 1)
         gate_product("phi", 7, 0)
+        quantize_feat("phi", 5)
+        round_y(3, 0, 1)
+        y_matmuls(4, 1)
+        turn_y(2, 0)
+        y_matmuls(5, 0)
+        group_y(1, 1, 1)
+        gate_product("phi", 7, 1)
+        round_y(3, 1, 2)
+        group_feat("phi", 6, 1)
         scale_y(4, 1)
-        round_y(4, 0, 1)
-        group_y(2, 1, 1)
         scale_y(5, 0)
+        turn_y(2, 1)
+        group_y(2, 0, 1)
         quantize_y(1, 0)
         quantize_y(1, 1)
-        gate_product("phi", 7, 1)
-        y_matmuls(5, 1)
         quantize_feat("phi", 6)
+        round_y(4, 0, 1)
+        y_matmuls(5, 1)
         turn_y(3, 0)
         y_matmuls(6, 0)
-        group_feat("phi", 7, 1)
+        group_y(2, 1, 1)
         round_y(4, 1, 2)
-        group_y(3, 0, 1)
-        turn_y(3, 1)
         scale_y(5, 1)
-        round_y(5, 0, 1)
-        group_y(3, 1, 1)
+        group_feat("phi", 7, 1)
         scale_y(6, 0)
+        turn_y(3, 1)
+        group_y(3, 0, 1)
         quantize_y(2, 0)
         quantize_y(2, 1)
+        quantize_feat("phi", 7)
+        round_y(5, 0, 1)
         y_matmuls(6, 1)
         turn_y(4, 0)
-        quantize_feat("phi", 7)
         y_matmuls(7, 0)
+        group_y(3, 1, 1)
         round_y(5, 1, 2)
-        group_y(4, 0, 1)
-        turn_y(4, 1)
         scale_y(6, 1)
-        round_y(6, 0, 1)
-        group_y(4, 1, 1)
         scale_y(7, 0)
+        turn_y(4, 1)
+        group_y(4, 0, 1)
         quantize_y(3, 0)
         quantize_y(3, 1)
+        round_y(6, 0, 1)
         y_matmuls(7, 1)
         turn_y(5, 0)
+        group_y(4, 1, 1)
         round_y(6, 1, 2)
-        group_y(5, 0, 1)
-        turn_y(5, 1)
         scale_y(7, 1)
-        round_y(7, 0, 0)
-        group_y(5, 1, 1)
+        turn_y(5, 1)
+        group_y(5, 0, 1)
         quantize_y(4, 0)
         quantize_y(4, 1)
+        round_y(7, 0, 0)
         turn_y(6, 0)
+        group_y(5, 1, 1)
         round_y(7, 1, 1)
-        group_y(6, 0, 1)
         turn_y(6, 1)
-        round_y(8, 0, 1)
-        group_y(6, 1, 1)
+        group_y(6, 0, 1)
         quantize_y(5, 0)
         quantize_y(5, 1)
+        round_y(8, 0, 0)
         turn_y(7, 0)
-        group_y(7, 0, 0)
+        group_y(6, 1, 1)
         turn_y(7, 1)
-        group_y(7, 1, 1)
+        group_y(7, 0, 1)
         quantize_y(6, 0)
         quantize_y(6, 1)
+        group_y(7, 1, 0)
         quantize_y(7, 0)
         quantize_y(7, 1)

from contextlib import ExitStack

import concourse.mybir as mybir
from concourse.masks import make_identity

T, K, J, F, N = 2048, 1024, 512, 512, 1024
FLOPS = 2 * (2 * T * K * F + 2 * N * J * F + T * F * N)

F32 = mybir.dt.float32
BF16 = mybir.dt.bfloat16
I32 = mybir.dt.int32
U32 = mybir.dt.uint32
U8 = mybir.dt.uint8
FP8 = mybir.dt.float8_e4m3fn
FP8X4 = mybir.dt.float8_e4m3fn_x4
FP4X4 = mybir.dt.float4_e2m1fn_x4
ACT = mybir.ActivationFunctionType
MULT = mybir.AluOpType.mult
ADD = mybir.AluOpType.add

P = 128
PACK = 4
K_PASS = P * PACK
W = 256
CHUNKS = T // W
GOAL_GROUPS = N // W
ROWS = W // P
SCALE_BLOCK = 128
LAST_SCALES = 2


def tile_goal_conditioned_critic_b8_kernel(
    tc, X_bytes, X_scale, G_words, G_scales, Wa, Wb, Va, Vb, phi_gain, psi_gain, goal_scale, out_0, out_1, out_2
):
    nc = tc.nc
    with ExitStack() as ctx:
        keep = ctx.enter_context(tc.tile_pool(name="keep", bufs=1))
        work = ctx.enter_context(tc.tile_pool(name="work", bufs=2))
        psum = ctx.enter_context(tc.psum_pool(name="psum", bufs=8))
        ctx.enter_context(tc.manual_schedule())

        x_raw, w_raw, w_grouped, w_codes, w_scales = {}, {}, {}, {}, {}
        x_wide, x_bank, x_grouped, x_codes, x_scales = {}, {}, {}, {}, {}
        gate_bank, tanh_part, sigmoid_part, feat_planes, feat_grouped = {}, {}, {}, {}, {}
        phi_codes, phi_scales = {}, {}
        y_sorted = {}
        y_bank, y_half, yt_bank, yt_grouped = {}, {}, {}, {}
        y_rows = keep.tile([P, CHUNKS * ROWS * N], F32, name="y_rows")

        warm = keep.tile([P, 1], F32, name="warm")
        nc.vector.memset(warm[:], 0.0)
        nc.scalar.activation(out=warm[:], in_=warm[:], func=ACT.Sigmoid)

        ident = keep.tile([P, P], F32, name="ident")
        make_identity(nc, ident[:])
        g_scales = keep.tile([P, N], U8, name="g_scales", align_bytes=64)
        nc.vector.memset(g_scales[:].bitcast(I32), 0)

        def load_x(c):
            x_raw[c] = keep.tile([P, ROWS * K], U8, name="x_raw%d" % c)
            nc.sync.dma_start(out=x_raw[c][:], in_=X_bytes[c * W : (c + 1) * W, :].rearrange("(p i) k -> p (i k)", i=ROWS))

        weights = {"va": Va, "vb": Vb, "wa": Wa, "wb": Wb}

        def load_w(name, g):
            w_raw[name, g] = keep.tile([P, PACK, F], BF16, name="raw_%s%d" % (name, g))
            nc.sync.dma_start(
                out=w_raw[name, g][:],
                in_=weights[name][g * K_PASS : (g + 1) * K_PASS, :].rearrange("(p j) f -> p j f", j=PACK),
            )

        x_scale_first = keep.tile([P, 1, ROWS * K // SCALE_BLOCK], F32, name="x_scale_first")
        x_scale_rest = keep.tile([P, CHUNKS - 1, ROWS * K // SCALE_BLOCK], F32, name="x_scale_rest")
        g_words = keep.tile([P, 2 * N], U8, name="g_words", align_bytes=64)
        gain_raw = {"phi": keep.tile([P, PACK], BF16, name="phi_gain_raw"), "psi": keep.tile([P, PACK], BF16, name="psi_gain_raw")}
        gain = {"phi": keep.tile([P, PACK], F32, name="phi_gain"), "psi": keep.tile([P, PACK], F32, name="psi_gain")}
        goal_row = keep.tile([P, N], BF16, name="goal_row")

        scale_rows = X_scale.rearrange("(c p i) j -> p c (i j)", p=P, i=ROWS)

        def load_small(what):
            if what == "scale_first":
                nc.sync.dma_start(out=x_scale_first[:], in_=scale_rows[:, 0:1, :])
            elif what == "scale_rest":
                nc.sync.dma_start(out=x_scale_rest[:], in_=scale_rows[:, 1:, :])
            elif what == "g_scales":
                for q in range(4):
                    nc.sync.dma_start(
                        out=g_scales[32 * q : 32 * q + 4, :].bitcast(I32), in_=G_scales[0, 4 * q : 4 * q + 4, :].bitcast(I32)
                    )
            elif what == "g_words":
                nc.sync.dma_start(out=g_words[:], in_=G_words[0])
            elif what == "gains":
                nc.sync.dma_start(out=gain_raw["psi"][:], in_=psi_gain.rearrange("o (p t) -> p (o t)", t=PACK))
                nc.sync.dma_start(out=gain_raw["phi"][:], in_=phi_gain.rearrange("o (p t) -> p (o t)", t=PACK))
            else:
                nc.sync.dma_start(out=goal_row[:], in_=goal_scale.rearrange("o n -> (o n)").partition_broadcast(P))

        psi_codes = [keep.tile([P, N // 2], U32, name="psi_codes%d" % h, align_bytes=64) for h in range(2)]
        psi_scales = [keep.tile([P, N // 2], U8, name="psi_scales%d" % h, align_bytes=64) for h in range(2)]
        first_cols = (CHUNKS - LAST_SCALES) * W
        yt_scales = [
            keep.tile([P, 2, first_cols], U8, name="yt_scales_first", align_bytes=64),
            keep.tile([P, 2, T - first_cols], U8, name="yt_scales_last", align_bytes=64),
        ]

        def group_w(name, g, on_scalar):
            w_grouped[name, g] = work.tile([P, PACK * F], BF16, name="w_grouped", bufs=3, align_bytes=64)
            dst = w_grouped[name, g][:].rearrange("p (t m j) -> p m j t", t=PACK, j=PACK)
            src = w_raw[name, g][:].rearrange("p j (m t) -> p m j t", t=PACK)
            if on_scalar:
                nc.scalar.copy(out=dst, in_=src)
            else:
                nc.vector.tensor_copy(out=dst, in_=src)

        def quantize_w(name, g):
            w_codes[name, g] = keep.tile([P, F], U32, name="codes_%s%d" % (name, g), align_bytes=64)
            w_scales[name, g] = keep.tile([P, F], U8, name="scales_%s%d" % (name, g), align_bytes=64)
            nc.vector.quantize_mx(out=w_codes[name, g][:].bitcast(FP8X4), scales=w_scales[name, g][:], in_=w_grouped[name, g][:])

        def widen_gain(name):
            nc.vector.tensor_copy(out=gain[name][:], in_=gain_raw[name][:])

        def widen_x(c, g, on_scalar=True):
            for i in range(ROWS):
                x_wide[c, g, i] = work.tile([P, K_PASS], BF16, name="x_wide", bufs=8)
                for b in range(K_PASS // SCALE_BLOCK):
                    j = (i * K + g * K_PASS) // SCALE_BLOCK + b
                    dst = x_wide[c, g, i][:, b * SCALE_BLOCK : (b + 1) * SCALE_BLOCK]
                    src = x_raw[c][:, j * SCALE_BLOCK : (j + 1) * SCALE_BLOCK].bitcast(FP8)
                    scale = x_scale_first[:, 0, j : j + 1] if c == 0 else x_scale_rest[:, c - 1, j : j + 1]
                    if on_scalar:
                        nc.scalar.activation(out=dst, in_=src, func=ACT.Copy, scale=scale)
                    else:
                        nc.vector.tensor_scalar(out=dst, in0=src, scalar1=scale, scalar2=None, op0=MULT)

        def turn_x(c, g):
            x_bank[c, g] = psum.tile([P, ROWS, 2, P], F32, name="bank")
            for i in range(ROWS):
                words = x_wide[c, g, i][:].bitcast(F32)
                for u in range(2):
                    nc.tensor.transpose(x_bank[c, g][:, i, u, :], words[:, u : 2 * P : 2], ident[:])

        def group_x(c, g, on_scalar=True):
            if g == 0:
                x_grouped[c] = work.tile([P, 2, ROWS, P, 2], F32, name="x_grouped", align_bytes=64)
            copy = nc.scalar.copy if on_scalar else nc.vector.tensor_copy
            copy(out=x_grouped[c][:, g], in_=x_bank[c, g][:].rearrange("p i u r -> p i r u"))

        def quantize_x(c):
            x_codes[c] = work.tile([P, 2 * W], U32, name="x_codes", bufs=3, align_bytes=64)
            x_scales[c] = work.tile([P, 2 * W], U8, name="x_scales", bufs=3, align_bytes=64)
            nc.vector.quantize_mx(
                out=x_codes[c][:].bitcast(FP8X4),
                scales=x_scales[c][:],
                in_=x_grouped[c][:].rearrange("p g i r u -> p (g i r u)").bitcast(BF16),
            )

        def gate_matmuls(kind, c, h):
            for name in ("va", "vb") if kind == "psi" else ("wa", "wb"):
                bank = psum.tile([P, 2, W], F32, name="bank")
                gate_bank[kind, c, h, name[1]] = bank
                for s in range(2):
                    cols = slice((2 * h + s) * P, (2 * h + s + 1) * P)
                    passes = 1 if kind == "psi" else 2
                    for g in range(passes):
                        if kind == "psi":
                            rhs = g_words[:, 2 * c * W : 2 * (c + 1) * W].bitcast(FP4X4)
                            rhs_scale = g_scales[:, c * W : (c + 1) * W]
                        else:
                            rhs = x_codes[c][:, g * W : (g + 1) * W].bitcast(FP8X4)
                            rhs_scale = x_scales[c][:, g * W : (g + 1) * W]
                        nc.tensor.matmul_mx(
                            out=bank[:, s, :],
                            lhsT=w_codes[name, g][:, cols].bitcast(FP8X4),
                            lhsT_scale=w_scales[name, g][:, cols],
                            rhs=rhs,
                            rhs_scale=rhs_scale,
                            start=(g == 0),
                            stop=(g == passes - 1),
                        )

        def gate_functions(kind, c, h):
            tanh_part[kind, c, h] = work.tile([P, 2, W], F32, name="tanh_part", bufs=4)
            sigmoid_part[kind, c, h] = work.tile([P, 2, W], F32, name="sigmoid_part", bufs=4)
            nc.scalar.activation(out=tanh_part[kind, c, h][:], in_=gate_bank[kind, c, h, "a"][:], func=ACT.Tanh)
            nc.scalar.activation(out=sigmoid_part[kind, c, h][:], in_=gate_bank[kind, c, h, "b"][:], func=ACT.Sigmoid)

        def gate_product(kind, c, h):
            if h == 0:
                feat_planes[kind, c] = work.tile([P, PACK, W], BF16, name="feat_planes")
            for s in range(2):
                t = 2 * h + s
                nc.vector.scalar_tensor_tensor(
                    out=feat_planes[kind, c][:, t, :],
                    in0=tanh_part[kind, c, h][:, s, :],
                    scalar=gain[kind][:, t : t + 1],
                    in1=sigmoid_part[kind, c, h][:, s, :],
                    op0=MULT,
                    op1=MULT,
                )

        def group_feat(kind, c, on_scalar=False):
            feat_grouped[kind, c] = work.tile([P, W * PACK], BF16, name="feat_grouped", align_bytes=64)
            copy = nc.scalar.copy if on_scalar else nc.vector.tensor_copy
            copy(
                out=feat_grouped[kind, c][:].rearrange("p (r i t) -> p r t i", i=4, t=PACK),
                in_=feat_planes[kind, c][:].rearrange("p t (r i) -> p r t i", i=4),
            )

        def quantize_feat(kind, c):
            if kind == "psi":
                cols = slice((c % 2) * W, (c % 2 + 1) * W)
                codes, scales = psi_codes[c // 2][:, cols], psi_scales[c // 2][:, cols]
            else:
                phi_codes[c] = work.tile([P, W], U32, name="phi_codes", align_bytes=64)
                phi_scales[c] = work.tile([P, W], U8, name="phi_scales", align_bytes=64)
                codes, scales = phi_codes[c][:], phi_scales[c][:]
            nc.vector.quantize_mx(out=codes.bitcast(FP8X4), scales=scales, in_=feat_grouped[kind, c][:])

        def y_matmuls(c, i):
            for h in range(2):
                y_bank[c, i, h] = psum.tile([P, N // 2], F32, name="bank")
                nc.tensor.matmul_mx(
                    out=y_bank[c, i, h][:],
                    lhsT=phi_codes[c][:, i * P : (i + 1) * P].bitcast(FP8X4),
                    lhsT_scale=phi_scales[c][:, i * P : (i + 1) * P],
                    rhs=psi_codes[h][:].bitcast(FP8X4),
                    rhs_scale=psi_scales[h][:],
                    start=True,
                    stop=True,
                )

        def scale_y(c, i):
            first = (c * ROWS + i) * N
            for h in range(2):
                cols = slice(h * K_PASS, (h + 1) * K_PASS)
                nc.vector.tensor_tensor(
                    out=y_rows[:, first + cols.start : first + cols.stop], in0=y_bank[c, i, h][:], in1=goal_row[:, cols], op=MULT
                )
            nc.sync.dma_start(
                out=out_0[c * W : (c + 1) * W, :].rearrange("(p i) n -> p i n", i=ROWS)[:, i, :], in_=y_rows[:, first : first + N]
            )

        def round_y(c, i, engine):
            r = c * ROWS + i
            y_half[r] = work.tile([P, N], BF16, name="y_half", bufs=5)
            first, last = max(r * N - K_PASS, 0), min(r * N + K_PASS, CHUNKS * ROWS * N)
            dst = y_half[r][:, first - (r * N - K_PASS) : last - (r * N - K_PASS)]
            src = y_rows[:, first:last]
            if engine == 2:
                nc.gpsimd.tensor_scalar(out=dst, in0=src, scalar1=1.0, scalar2=0.0, op0=MULT, op1=ADD)
            else:
                copy = nc.scalar.copy if engine == 1 else nc.vector.tensor_copy
                copy(
                    out=dst.rearrange("p (h u m e) -> p h m u e", u=2, m=P, e=2),
                    in_=src.rearrange("p (h m u e) -> p h m u e", u=2, m=P, e=2),
                )
            y_sorted[r] = engine != 2

        def turn_y(c, g):
            yt_bank[c, g] = psum.tile([P, ROWS, 2, P], F32, name="bank")
            for i in range(ROWS):
                words = y_half[c * ROWS + i + g][:].bitcast(F32)
                for u in range(2):
                    first = (1 - g) * 2 * P
                    if y_sorted[c * ROWS + i + g]:
                        src = words[:, first + u * P : first + (u + 1) * P]
                    else:
                        src = words[:, first + u : first + 2 * P : 2]
                    nc.tensor.transpose(yt_bank[c, g][:, i, u, :], src, ident[:])

        def group_y(c, g, on_scalar=True):
            yt_grouped[c, g] = work.tile([P, P, ROWS, 2], F32, name="yt_grouped", bufs=4, align_bytes=64)
            copy = nc.scalar.copy if on_scalar else nc.vector.tensor_copy
            copy(out=yt_grouped[c, g][:], in_=yt_bank[c, g][:].rearrange("p i u r -> p r i u"))

        def quantize_y(c, g):
            yt_codes = work.tile([P, W], U32, name="yt_codes", bufs=6, align_bytes=64)
            part = int(c * W >= first_cols)
            first = c * W - part * first_cols
            nc.vector.quantize_mx(
                out=yt_codes[:].bitcast(FP8X4),
                scales=yt_scales[part][:, g, first : first + W],
                in_=yt_grouped[c, g][:].rearrange("p r i u -> p (r i u)").bitcast(BF16),
            )
            nc.sync.dma_start(
                out=out_1[g, :, c * W : (c + 1) * W, :].rearrange("p m t -> p (m t)").bitcast(I32), in_=yt_codes[:].bitcast(I32)
            )
            if g == 1 and (c + 1) * W in (first_cols, T):
                cols = slice(part * first_cols, (c + 1) * W)
                for q in range(4):
                    queue = nc.scalar if part == 1 and q < 3 else nc.sync
                    queue.dma_start(
                        out=out_2[:, 4 * q : 4 * q + 4, cols].rearrange("g r m -> r g m").bitcast(I32),
                        in_=yt_scales[part][32 * q : 32 * q + 4].bitcast(I32),
                    )

        load_w("vb", 0)
        load_small("gains")
        load_small("scale_first")
        load_x(0)
        load_w("va", 0)
        load_w("wb", 0)
        load_w("wa", 0)
        load_small("g_words")
        load_small("g_scales")
        load_w("wa", 1)
        load_small("scale_rest")
        load_x(1)
        load_x(2)
        load_w("wb", 1)
        load_x(3)
        load_x(4)
        load_x(5)
        load_x(6)
        load_x(7)
        load_small("goal_row")
        group_w("vb", 0, 0)
        quantize_w("vb", 0)
        widen_x(0, 0, 1)
        group_w("va", 0, 0)
        widen_x(0, 1, 1)
        group_w("wb", 0, 1)
        widen_gain("psi")
        quantize_w("va", 0)
        group_w("wa", 0, 0)
        widen_gain("phi")
        quantize_w("wa", 0)
        quantize_w("wb", 0)
        gate_matmuls("psi", 0, 0)
        gate_matmuls("psi", 0, 1)
        gate_functions("psi", 0, 0)
        gate_functions("psi", 0, 1)
        group_w("wa", 1, 0)
        gate_matmuls("psi", 1, 0)
        gate_product("psi", 0, 0)
        gate_matmuls("psi", 1, 1)
        gate_functions("psi", 1, 0)
        gate_functions("psi", 1, 1)
        gate_product("psi", 0, 1)
        group_w("wb", 1, 0)
        widen_x(1, 0, 0)
        gate_matmuls("psi", 2, 0)
        gate_product("psi", 1, 0)
        gate_matmuls("psi", 2, 1)
        gate_functions("psi", 2, 0)
        gate_functions("psi", 2, 1)
        gate_product("psi", 1, 1)
        widen_x(1, 1, 0)
        turn_x(0, 0)
        turn_x(0, 1)
        group_feat("psi", 0, 0)
        group_x(0, 0, 1)
        group_x(0, 1, 1)
        widen_x(2, 0, 0)
        quantize_w("wa", 1)
        gate_matmuls("psi", 3, 0)
        gate_product("psi", 2, 0)
        gate_matmuls("psi", 3, 1)
        gate_functions("psi", 3, 0)
        quantize_x(0)
        gate_functions("psi", 3, 1)
        quantize_feat("psi", 0)
        gate_product("psi", 2, 1)
        widen_x(2, 1, 1)
        quantize_w("wb", 1)
        turn_x(1, 0)
        turn_x(1, 1)
        group_x(1, 0, 1)
        group_x(1, 1, 1)
        widen_x(3, 0, 0)
        group_feat("psi", 1, 0)
        quantize_x(1)
        widen_x(3, 1, 0)
        turn_x(2, 0)
        turn_x(2, 1)
        gate_product("psi", 3, 0)
        quantize_feat("psi", 1)
        group_x(2, 0, 1)
        group_x(2, 1, 1)
        gate_product("psi", 3, 1)
        widen_x(4, 0, 1)
        group_feat("psi", 2, 0)
        quantize_x(2)
        widen_x(4, 1, 0)
        gate_matmuls("phi", 0, 0)
        turn_x(3, 0)
        turn_x(3, 1)
        gate_functions("phi", 0, 0)
        group_x(3, 0, 1)
        group_x(3, 1, 1)
        widen_x(5, 0, 0)
        gate_matmuls("phi", 0, 1)
        quantize_feat("psi", 2)
        gate_functions("phi", 0, 1)
        gate_matmuls("phi", 1, 0)
        quantize_x(3)
        gate_product("phi", 0, 0)
        widen_x(5, 1, 0)
        gate_functions("phi", 1, 0)
        turn_x(4, 0)
        turn_x(4, 1)
        group_feat("psi", 3, 0)
        gate_matmuls("phi", 1, 1)
        gate_product("phi", 0, 1)
        group_x(4, 0, 1)
        group_x(4, 1, 1)
        widen_x(6, 0, 0)
        gate_functions("phi", 1, 1)
        gate_matmuls("phi", 2, 0)
        gate_product("phi", 1, 0)
        gate_functions("phi", 2, 0)
        quantize_x(4)
        quantize_feat("psi", 3)
        widen_x(6, 1, 1)
        gate_matmuls("phi", 2, 1)
        gate_product("phi", 1, 1)
        turn_x(5, 0)
        turn_x(5, 1)
        group_feat("phi", 0, 0)
        gate_functions("phi", 2, 1)
        group_x(5, 0, 1)
        group_x(5, 1, 1)
        gate_matmuls("phi", 3, 0)
        widen_x(7, 0, 0)
        gate_product("phi", 2, 0)
        quantize_feat("phi", 0)
        gate_functions("phi", 3, 0)
        gate_matmuls("phi", 3, 1)
        gate_product("phi", 2, 1)
        y_matmuls(0, 0)
        group_feat("phi", 1, 1)
        quantize_x(5)
        gate_functions("phi", 3, 1)
        widen_x(7, 1, 1)
        scale_y(0, 0)
        gate_matmuls("phi", 4, 0)
        turn_x(6, 0)
        turn_x(6, 1)
        gate_product("phi", 3, 0)
        quantize_feat("phi", 1)
        gate_functions("phi", 4, 0)
        group_x(6, 0, 1)
        group_x(6, 1, 1)
        y_matmuls(0, 1)
        y_matmuls(1, 0)
        gate_matmuls("phi", 4, 1)
        gate_product("phi", 3, 1)
        group_feat("phi", 2, 0)
        gate_functions("phi", 4, 1)
        scale_y(0, 1)
        scale_y(1, 0)
        gate_matmuls("phi", 5, 0)
        quantize_x(6)
        gate_product("phi", 4, 0)
        quantize_feat("phi", 2)
        gate_functions("phi", 5, 0)
        turn_x(7, 0)
        round_y(0, 0, 1)
        turn_x(7, 1)
        y_matmuls(1, 1)
        y_matmuls(2, 0)
        gate_matmuls("phi", 5, 1)
        gate_product("phi", 4, 1)
        group_x(7, 0, 1)
        group_x(7, 1, 1)
        round_y(0, 1, 2)
        group_feat("phi", 3, 1)
        gate_functions("phi", 5, 1)
        scale_y(1, 1)
        scale_y(2, 0)
        gate_matmuls("phi", 6, 0)
        gate_product("phi", 5, 0)
        quantize_feat("phi", 3)
        gate_functions("phi", 6, 0)
        round_y(1, 0, 0)
        y_matmuls(2, 1)
        turn_y(0, 0)
        quantize_x(7)
        y_matmuls(3, 0)
        gate_matmuls("phi", 6, 1)
        gate_product("phi", 5, 1)
        round_y(1, 1, 2)
        group_feat("phi", 4, 1)
        gate_functions("phi", 6, 1)
        scale_y(2, 1)
        scale_y(3, 0)
        turn_y(0, 1)
        gate_matmuls("phi", 7, 0)
        group_y(0, 0, 1)
        gate_product("phi", 6, 0)
        quantize_feat("phi", 4)
        gate_functions("phi", 7, 0)
        round_y(2, 0, 1)
        y_matmuls(3, 1)
        turn_y(1, 0)
        y_matmuls(4, 0)
        group_y(0, 1, 1)
        gate_matmuls("phi", 7, 1)
        gate_product("phi", 6, 1)
        round_y(2, 1, 2)
        group_feat("phi", 5, 1)
        gate_functions("phi", 7, 1)
        scale_y(3, 1)
        scale_y(4, 0)
        turn_y(1, 1)
        group_y(1, 0, 1)
        quantize_y(0, 0)
        quantize_y(0, 1)
        gate_product("phi", 7, 0)
        quantize_feat("phi", 5)
        round_y(3, 0, 1)
        y_matmuls(4, 1)
        turn_y(2, 0)
        y_matmuls(5, 0)
        group_y(1, 1, 1)
        gate_product("phi", 7, 1)
        round_y(3, 1, 2)
        group_feat("phi", 6, 1)
        scale_y(4, 1)
        scale_y(5, 0)
        turn_y(2, 1)
        group_y(2, 0, 1)
        quantize_y(1, 0)
        quantize_y(1, 1)
        quantize_feat("phi", 6)
        round_y(4, 0, 1)
        y_matmuls(5, 1)
        turn_y(3, 0)
        y_matmuls(6, 0)
        group_y(2, 1, 1)
        round_y(4, 1, 2)
        scale_y(5, 1)
        group_feat("phi", 7, 1)
        scale_y(6, 0)
        turn_y(3, 1)
        group_y(3, 0, 1)
        quantize_y(2, 0)
        quantize_y(2, 1)
        quantize_feat("phi", 7)
        round_y(5, 0, 1)
        y_matmuls(6, 1)
        turn_y(4, 0)
        y_matmuls(7, 0)
        group_y(3, 1, 1)
        round_y(5, 1, 2)
        scale_y(6, 1)
        scale_y(7, 0)
        turn_y(4, 1)
        group_y(4, 0, 1)
        quantize_y(3, 0)
        quantize_y(3, 1)
        round_y(6, 0, 1)
        y_matmuls(7, 1)
        turn_y(5, 0)
        group_y(4, 1, 1)
        round_y(6, 1, 2)
        scale_y(7, 1)
        turn_y(5, 1)
        group_y(5, 0, 1)
        quantize_y(4, 0)
        quantize_y(4, 1)
        round_y(7, 0, 0)
        turn_y(6, 0)
        group_y(5, 1, 1)
        round_y(7, 1, 1)
        turn_y(6, 1)
        group_y(6, 0, 1)
        quantize_y(5, 0)
        quantize_y(5, 1)
        round_y(8, 0, 0)
        turn_y(7, 0)
        group_y(6, 1, 1)
        turn_y(7, 1)
        group_y(7, 0, 1)
        quantize_y(6, 0)
        quantize_y(6, 1)
        group_y(7, 1, 0)
        quantize_y(7, 0)
        quantize_y(7, 1)
